import numpy as np
import ml_dtypes


def mxq(x, axis, fmt="e4m3"):
    dtype, down = {"e4m3": (ml_dtypes.float8_e4m3fn, 7), "e5m2": (ml_dtypes.float8_e5m2, 14)}[fmt]
    v = np.moveaxis(np.asarray(x, np.float32).astype(ml_dtypes.bfloat16).astype(np.float64), axis, -1)
    blocks = v.reshape(v.shape[:-1] + (-1, 32))
    amax = np.abs(blocks).max(-1, keepdims=True)
    byte = np.maximum(np.where(amax > 0, np.frexp(amax)[1] - 1 + 127, 0) - down, 1)
    scale = np.exp2(byte - 127.0)
    codes = (blocks / scale).astype(np.float32).astype(dtype).astype(np.float64)
    return np.moveaxis((codes * scale).reshape(v.shape), -1, axis)


WIDE = False


def mx_kscale(k):
    if not WIDE:
        return np.ones(k)
    levels = np.array([10, -10, 5, -5, 0])
    if k % 512:
        return np.exp2(np.random.permutation(np.resize(levels, k // 32))).repeat(32)
    a = np.empty((k // 512, 16))
    for p in range(k // 512):
        a[p, :8] = np.random.permutation(np.resize(levels, 8))
        for g in range(8):
            far = levels[np.abs(levels - a[p, g]) >= 10]
            a[p, g + 8] = far[np.random.randint(len(far))]
    return np.exp2(a.ravel()).repeat(32)


def f64(x):
    return np.asarray(x).astype(np.float64)


def striped(idx):
    return np.tile(idx.reshape(-1, 16).T, (8, 1)).astype(np.uint16)


def unstriped(offs):
    return offs[:16].T.reshape(-1).astype(np.int64)


E2M1 = np.array([0.0, 0.5, 1.0, 1.5, 2.0, 3.0, 4.0, 6.0, -0.0, -0.5, -1.0, -1.5, -2.0, -3.0, -4.0, -6.0])


def pack_weight(w, fmt):
    k, n = w.shape
    w = f64(np.asarray(w, np.float32).astype(ml_dtypes.bfloat16)).reshape(k // 32, 32, n)
    amax = np.abs(w).max(1)
    if fmt == "e4m3":
        byte = np.frexp(amax)[1] - 1 + 127 - 7
    else:
        mant, ex = np.frexp(amax / 6.0)
        byte = np.where(mant > 0.5, ex, ex - 1) + 127
    byte = np.clip(np.where(amax > 0, byte, 1), 1, 254)
    scaled = (w * np.exp2(127.0 - byte)[:, None, :]).reshape(k, n).astype(np.float32)
    by_word = np.ascontiguousarray(scaled.reshape(k // 512, 128, 4, n).transpose(0, 1, 3, 2))
    if fmt == "e4m3":
        words = by_word.astype(ml_dtypes.float8_e4m3fn).view(np.uint8)
    else:
        c = by_word.astype(ml_dtypes.float4_e2m1fn).view(np.uint8) & 0xF
        words = (c[..., 0::2] | (c[..., 1::2] << 4)).reshape(k // 512, 128, 2 * n)
    return np.ascontiguousarray(words), np.ascontiguousarray(byte.astype(np.uint8).reshape(k // 512, 16, n))


def unpack_weight(words, scales, fmt):
    g, _, n = scales.shape
    words = np.ascontiguousarray(words).reshape(g, 128, n, -1)
    if fmt == "e4m3":
        vals = words.view(ml_dtypes.float8_e4m3fn).astype(np.float64)
    else:
        nib = np.empty((g, 128, n, 4), np.uint8)
        nib[..., 0::2] = words & 0xF
        nib[..., 1::2] = words >> 4
        vals = E2M1[nib]
    vals = vals * np.repeat(np.exp2(scales.astype(np.float64) - 127.0), 8, axis=1)[..., None]
    return vals.transpose(0, 1, 3, 2).reshape(g * 512, n)


def silu(v):
    return v / (1.0 + np.exp(-np.maximum(v, -700.0)))


K, T, E, C, H, N = 512, 4096, 8, 256, 512, 256
R = 2


def by_expert(wq, xq):
    return np.concatenate([wq[e].T @ xq[:, e * C:(e + 1) * C] for e in range(E)], axis=1)


def setup_inputs():
    n = np.random.standard_normal
    s = mx_kscale(K)[:, None]
    u = mx_kscale(H)
    slot_token = np.concatenate([r * (T // R) + np.random.permutation(T // R)[:C // R] for e in range(E) for r in range(R)])
    w1 = [pack_weight(m, "e2m1") for m in n((E, K, H)) / np.sqrt(K) / s[None] * u[None, None, :]]
    w2 = [pack_weight(m, "e2m1") for m in n((E, H, N)) / np.sqrt(H) / u[None, :, None]]
    x = pack_weight(n((K, T)) * s, "e4m3")
    return {
        "x_words": x[0],
        "x_scales": x[1],
        "w1_words": np.stack([m[0] for m in w1]),
        "w1_scales": np.stack([m[1] for m in w1]),
        "w2_words": np.stack([m[0] for m in w2]),
        "w2_scales": np.stack([m[1] for m in w2]),
        "offs": striped(slot_token),
    }


def reference(x_words, x_scales, w1_words, w1_scales, w2_words, w2_scales, offs):
    idx = unstriped(offs)
    w1 = np.stack([unpack_weight(w1_words[e], w1_scales[e], "e2m1") for e in range(E)])
    w2 = np.stack([unpack_weight(w2_words[e], w2_scales[e], "e2m1") for e in range(E)])
    xq = unpack_weight(x_words, x_scales, "e4m3")[:, idx]
    h = silu(by_expert(w1, xq))
    y = by_expert(w2, mxq(h, 0, "e4m3"))
    return y.reshape(N, E, R, C // R).transpose(0, 2, 1, 3).reshape(N, E * C)

@@ -1,0 +1,193 @@
+from contextlib import ExitStack
+
+import concourse.mybir as mybir
+
+F32 = mybir.dt.float32
+BF16 = mybir.dt.bfloat16
+I32 = mybir.dt.int32
+U32 = mybir.dt.uint32
+U16 = mybir.dt.uint16
+U8 = mybir.dt.uint8
+FP8X4 = mybir.dt.float8_e4m3fn_x4
+FP4X4 = mybir.dt.float4_e2m1fn_x4
+SILU = mybir.ActivationFunctionType.Silu
+
+P = 128
+PACK = 4
+K, T, E, C, H, N = 512, 4096, 8, 256, 512, 256
+RANKS = 2
+U = C // RANKS
+GATHER = 512
+EARLY = 2
+SCALAR_COPIES = 3
+FLOPS = 2 * E * C * (K * H + H * N)
+
+
+def tile_moe_pke_mlp_silu_kernel(tc, x_words, x_scales, w1_words, w1_scales, w2_words, w2_scales, offs, out):
+    nc = tc.nc
+    with ExitStack() as ctx:
+        keep = ctx.enter_context(tc.tile_pool(name="keep", bufs=1))
+        work = ctx.enter_context(tc.tile_pool(name="work", bufs=4))
+        psum_a = ctx.enter_context(tc.psum_pool(name="psum_a", bufs=4))
+        psum_y = ctx.enter_context(tc.psum_pool(name="psum_y", bufs=4))
+
+        offsets = keep.tile([P, E * C // 16], U16, name="offsets")
+        xw = keep.tile([P, T], I32, name="xw", align_bytes=64)
+        xs = keep.tile([P, T // 4], I32, name="xs", tag="slot_a", align_bytes=64)
+        s1_raw = keep.tile([P, H // 4], I32, name="s1_raw", align_bytes=64)
+        s_mid = keep.tile([P, (H + N) // 4], I32, name="s_mid", align_bytes=64)
+        planes = keep.tile([P, E, (H + N) // 4], I32, name="planes", align_bytes=64)
+        w1_early = keep.tile([P, EARLY, H // 2], I32, name="w1_early", tag="slot_w", align_bytes=64)
+        warm_in = keep.tile([P, 1], F32, name="warm_in")
+        warm_out = keep.tile([P, 1], F32, name="warm_out")
+
+        nc.vector.memset(xs[:], 0)
+        nc.vector.memset(warm_in[:], 0.0)
+        nc.vector.memset(planes[:], 0)
+
+        w1_hbm = w1_words.rearrange("e s p b -> p (e s) b").bitcast(I32)
+        w2_hbm = w2_words.rearrange("e s p b -> p (e s) b").bitcast(I32)
+        nc.sync.dma_start(offsets[:], offs)
+        nc.sync.dma_start(s1_raw[:], w1_scales.rearrange("e s q i -> q (e s) i").bitcast(I32))
+        nc.sync.dma_start(s_mid[:, H // 4 :], w2_scales.rearrange("e s q i -> q (e s) i").bitcast(I32))
+        nc.sync.dma_start(w1_early[:], w1_hbm[:, 0:EARLY, :])
+        nc.sync.dma_start(xw[:], x_words[0].rearrange("p t r -> p (t r)").bitcast(I32))
+        for q in range(4):
+            nc.scalar.dma_start(xs[32 * q : 32 * q + 4, :], x_scales[0, 4 * q : 4 * q + 4, :].bitcast(I32))
+        nc.scalar.activation(warm_out[:], warm_in[:], SILU)
+
+        nc.vector.tensor_copy(
+            s_mid[:, 0 : H // 4].bitcast(U8).rearrange("p (t m) -> p t m", t=PACK),
+            s1_raw[:].bitcast(U8).rearrange("p (m t) -> p t m", t=PACK),
+        )
+        for q in range(4):
+            queue = nc.scalar if q < 2 else nc.gpsimd
+            queue.dma_start(planes[32 * q : 32 * q + 4, :, :], s_mid[32 * q : 32 * q + 32, :])
+
+        w1p = {}
+
+        def permute(e, raw):
+            w1p[e] = keep.tile([P, H // 2], I32, name="w1p%d" % e, align_bytes=64)
+            nc.vector.tensor_copy(
+                w1p[e][:].bitcast(U16).rearrange("p (t m) -> p t m", t=PACK),
+                raw.bitcast(U16).rearrange("p (m t) -> p t m", t=PACK),
+            )
+
+        for e in range(EARLY):
+            permute(e, w1_early[:, e, :])
+
+        late = keep.tile([P, (E - EARLY) * H // 2 + E * N // 2], I32, name="late", tag="slot_w", align_bytes=64)
+        w1_late = late[:, 0 : (E - EARLY) * H // 2].rearrange("p (e b) -> p e b", b=H // 2)
+        w2 = late[:, (E - EARLY) * H // 2 :].rearrange("p (e b) -> p e b", b=N // 2)
+        nc.sync.dma_start(w1_late, w1_hbm[:, EARLY:E, :])
+        nc.sync.dma_start(w2, w2_hbm)
+
+        def list_cols(first, count):
+            return offsets[:, first // 16 : (first + count) // 16]
+
+        sg = {}
+        sg0 = keep.tile([P, GATHER], U8, name="sg0", tag="slot_b", align_bytes=64)
+        sg1 = keep.tile([P, GATHER], U8, name="sg1", tag="slot_c", align_bytes=64)
+        sg23 = keep.tile([P, 2 * GATHER], U8, name="sg23", align_bytes=64)
+        nc.vector.tensor_copy(sg0[:], xs[:].bitcast(U8).indirect(list_cols(0, GATHER)))
+        nc.vector.tensor_copy(sg1[:], xs[:].bitcast(U8).indirect(list_cols(GATHER, GATHER)))
+        nc.vector.tensor_copy(sg23[:], xs[:].bitcast(U8).indirect(list_cols(2 * GATHER, 2 * GATHER)))
+        sg = {0: sg0[:], 1: sg1[:], 2: sg23[:, 0:GATHER], 3: sg23[:, GATHER:]}
+
+        xg01 = keep.tile([P, 2 * GATHER], U32, name="xg01", tag="slot_a", align_bytes=64)
+        xg = {0: xg01[:, 0:GATHER], 1: xg01[:, GATHER:]}
+
+        def gather(c):
+            if c == 2:
+                xg[c] = keep.tile([P, GATHER], U32, name="xg2", tag="slot_b", align_bytes=64)[:]
+            if c == 3:
+                xg[c] = keep.tile([P, GATHER], U32, name="xg3", tag="slot_c", align_bytes=64)[:]
+            nc.vector.tensor_copy(xg[c], xw[:].bitcast(U32).indirect(list_cols(c * GATHER, GATHER)))
+
+        out_v = out.rearrange("(g p) (m c) -> g p m c", p=P, m=RANKS)
+        hidden = {}
+
+        def layer1(e):
+            c = e * C // GATHER
+            h = work.tile([P, C, PACK], BF16, name="h", align_bytes=64)
+            for m in range(RANKS):
+                c0 = (e * C) % GATHER + m * U
+                a = psum_a.tile([P, PACK, U], F32, name="a")
+                for t in range(PACK):
+                    nc.tensor.matmul_mx(
+                        out=a[:, t, :],
+                        lhsT=w1p[e][:, t * P // 2 : (t + 1) * P // 2].bitcast(FP4X4),
+                        lhsT_scale=planes[:, e, t * P // 4 : (t + 1) * P // 4].bitcast(U8),
+                        rhs=xg[c][:, c0 : c0 + U].bitcast(FP8X4),
+                        rhs_scale=sg[c][:, c0 : c0 + U],
+                        start=True,
+                        stop=True,
+                    )
+                nc.scalar.activation(h[:, m * U : (m + 1) * U, :], a[:].rearrange("p t u -> p u t"), SILU)
+            hidden[e] = h
+
+        def product2(e, g, hq, hs, y):
+            nc.tensor.matmul_mx(
+                out=y,
+                lhsT=w2[:, e, g * P // 2 : (g + 1) * P // 2].bitcast(FP4X4),
+                lhsT_scale=planes[:, e, (H + g * P) // 4 : (H + (g + 1) * P) // 4].bitcast(U8),
+                rhs=hq.bitcast(FP8X4),
+                rhs_scale=hs,
+                start=True,
+                stop=True,
+            )
+
+        def quantise(values, width):
+            hq = work.tile([P, width], U32, name="hq", align_bytes=64)
+            hs = work.tile([P, width], U8, name="hs", align_bytes=64)
+            nc.vector.quantize_mx(out=hq[:].bitcast(FP8X4), scales=hs[:], in_=values.rearrange("p c t -> p (c t)"))
+            return hq[:], hs[:]
+
+        def layer2(e):
+            hq, hs = quantise(hidden[e][:], C)
+            y = psum_y.tile([P, N // P, C], F32, name="y")
+            for g in range(N // P):
+                product2(e, g, hq, hs, y[:, g, :])
+            staged = work.tile([P, N // P, C], F32, name="staged")
+            if e < SCALAR_COPIES:
+                nc.scalar.copy(staged[:], y[:])
+            else:
+                nc.vector.tensor_copy(staged[:], y[:])
+            for g in range(N // P):
+                nc.sync.dma_start(
+                    out_v[g, :, :, e * U : (e + 1) * U],
+                    staged[:, g, :].rearrange("p (m u) -> p m u", m=RANKS),
+                )
+
+        def layer2_last(e):
+            for m in range(RANKS):
+                hq, hs = quantise(hidden[e][:, m * U : (m + 1) * U, :], U)
+                if m == 0:
+                    y = psum_y.tile([P, N // P, U], F32, name="y")
+                    staged = work.tile([P, N // P, U], F32, name="staged")
+                    for g in range(N // P):
+                        product2(e, g, hq, hs, y[:, g, :])
+                    nc.vector.tensor_copy(staged[:], y[:])
+                    nc.sync.dma_start(out_v[:, :, m, e * U : (e + 1) * U].rearrange("g p u -> p g u"), staged[:])
+                else:
+                    for g in range(N // P):
+                        y = psum_y.tile([P, U], F32, name="y")
+                        staged = work.tile([P, U], F32, name="staged")
+                        product2(e, g, hq, hs, y[:])
+                        if g == 0:
+                            nc.vector.tensor_copy(staged[:], y[:])
+                            nc.sync.dma_start(out_v[g, :, m, e * U : (e + 1) * U], staged[:])
+                        else:
+                            nc.scalar.copy(staged[:], y[:])
+                            nc.scalar.dma_start(out_v[g, :, m, e * U : (e + 1) * U], staged[:])
+
+        gather(0)
+        for e in range(E):
+            layer1(e)
+            if e % 2 == 0 and e + 2 < E:
+                gather(e // 2 + 1)
+            if e + EARLY < E:
+                permute(e + EARLY, w1_late[:, e, :])
+            if e >= 1:
+                layer2(e - 1)
+        layer2_last(E - 1)

@@ -17,9 +17,9 @@ PACK = 4
 K, T, E, C, H, N = 512, 4096, 8, 256, 512, 256
 RANKS = 2
 U = C // RANKS
-GATHER = 512
-EARLY = 2
-SCALAR_COPIES = 3
+G = N // P
+PAIR = 2 * C
+SCALAR_COPIES = 4
 FLOPS = 2 * E * C * (K * H + H * N)
 
 
@@ -35,91 +35,89 @@ def tile_moe_pke_mlp_silu_kernel(tc, x_words, x_scales, w1_words, w1_scales, w2_
         xw = keep.tile([P, T], I32, name="xw", align_bytes=64)
         xs = keep.tile([P, T // 4], I32, name="xs", tag="slot_a", align_bytes=64)
         s1_raw = keep.tile([P, H // 4], I32, name="s1_raw", align_bytes=64)
-        s_mid = keep.tile([P, (H + N) // 4], I32, name="s_mid", align_bytes=64)
-        planes = keep.tile([P, E, (H + N) // 4], I32, name="planes", align_bytes=64)
-        w1_early = keep.tile([P, EARLY, H // 2], I32, name="w1_early", tag="slot_w", align_bytes=64)
+        s1_mid = keep.tile([P, H // 4], I32, name="s1_mid", align_bytes=64)
+        s1 = keep.tile([P, E, H // 4], I32, name="s1", align_bytes=64)
+        s2 = keep.tile([P, E, N // 4], I32, name="s2", align_bytes=64)
+        w1_a = keep.tile([P, 2, H // 2], I32, name="w1_a", align_bytes=64)
+        w1_b = keep.tile([P, 2, H // 2], I32, name="w1_b", tag="slot_b", align_bytes=64)
+        w1_c = keep.tile([P, 4, H // 2], I32, name="w1_c", align_bytes=64)
+        w2 = keep.tile([P, E, N // 2], I32, name="w2", align_bytes=64)
         warm_in = keep.tile([P, 1], F32, name="warm_in")
         warm_out = keep.tile([P, 1], F32, name="warm_out")
 
         nc.vector.memset(xs[:], 0)
         nc.vector.memset(warm_in[:], 0.0)
-        nc.vector.memset(planes[:], 0)
+        nc.vector.memset(s1[:], 0)
+        nc.vector.memset(s2[:], 0)
 
         w1_hbm = w1_words.rearrange("e s p b -> p (e s) b").bitcast(I32)
         w2_hbm = w2_words.rearrange("e s p b -> p (e s) b").bitcast(I32)
+        s2_hbm = w2_scales.rearrange("e s q i -> q (e s) i").bitcast(I32)
         nc.sync.dma_start(offsets[:], offs)
         nc.sync.dma_start(s1_raw[:], w1_scales.rearrange("e s q i -> q (e s) i").bitcast(I32))
-        nc.sync.dma_start(s_mid[:, H // 4 :], w2_scales.rearrange("e s q i -> q (e s) i").bitcast(I32))
-        nc.sync.dma_start(w1_early[:], w1_hbm[:, 0:EARLY, :])
+        nc.sync.dma_start(w1_a[:], w1_hbm[:, 0:2, :])
+        for r in range(4):
+            nc.sync.dma_start(xs[r:P:32, :], x_scales[0, r:16:4, :].bitcast(I32))
         nc.sync.dma_start(xw[:], x_words[0].rearrange("p t r -> p (t r)").bitcast(I32))
-        for q in range(4):
-            nc.scalar.dma_start(xs[32 * q : 32 * q + 4, :], x_scales[0, 4 * q : 4 * q + 4, :].bitcast(I32))
         nc.scalar.activation(warm_out[:], warm_in[:], SILU)
 
         nc.vector.tensor_copy(
-            s_mid[:, 0 : H // 4].bitcast(U8).rearrange("p (t m) -> p t m", t=PACK),
+            s1_mid[:].bitcast(U8).rearrange("p (t m) -> p t m", t=PACK),
             s1_raw[:].bitcast(U8).rearrange("p (m t) -> p t m", t=PACK),
         )
-        for q in range(4):
-            queue = nc.scalar if q < 2 else nc.gpsimd
-            queue.dma_start(planes[32 * q : 32 * q + 4, :, :], s_mid[32 * q : 32 * q + 32, :])
+        for q in (0, 2, 1, 3):
+            nc.sync.dma_start(s1[32 * q : 32 * q + 4, :, :], s1_mid[32 * q : 32 * q + 32, :])
+        nc.sync.dma_start(w1_b[:], w1_hbm[:, 2:4, :])
+        nc.sync.dma_start(w2[:], w2_hbm)
+        for r in range(4):
+            nc.sync.dma_start(s2[r:P:32, :, :], s2_hbm[r:16:4, :, :])
+        nc.sync.dma_start(w1_c[:], w1_hbm[:, 4:E, :])
 
         w1p = {}
 
-        def permute(e, raw):
-            w1p[e] = keep.tile([P, H // 2], I32, name="w1p%d" % e, align_bytes=64)
+        def permute(pair, raw):
+            w1p[pair] = keep.tile([P, 2, H // 2], I32, name="w1p%d" % pair, align_bytes=64)
             nc.vector.tensor_copy(
-                w1p[e][:].bitcast(U16).rearrange("p (t m) -> p t m", t=PACK),
-                raw.bitcast(U16).rearrange("p (m t) -> p t m", t=PACK),
+                w1p[pair][:].bitcast(U16).rearrange("p e (t m) -> p e t m", t=PACK),
+                raw.bitcast(U16).rearrange("p e (m t) -> p e t m", t=PACK),
             )
-
-        for e in range(EARLY):
-            permute(e, w1_early[:, e, :])
-
-        late = keep.tile([P, (E - EARLY) * H // 2 + E * N // 2], I32, name="late", tag="slot_w", align_bytes=64)
-        w1_late = late[:, 0 : (E - EARLY) * H // 2].rearrange("p (e b) -> p e b", b=H // 2)
-        w2 = late[:, (E - EARLY) * H // 2 :].rearrange("p (e b) -> p e b", b=N // 2)
-        nc.sync.dma_start(w1_late, w1_hbm[:, EARLY:E, :])
-        nc.sync.dma_start(w2, w2_hbm)
 
         def list_cols(first, count):
             return offsets[:, first // 16 : (first + count) // 16]
 
-        sg = {}
-        sg0 = keep.tile([P, GATHER], U8, name="sg0", tag="slot_b", align_bytes=64)
-        sg1 = keep.tile([P, GATHER], U8, name="sg1", tag="slot_c", align_bytes=64)
-        sg23 = keep.tile([P, 2 * GATHER], U8, name="sg23", align_bytes=64)
-        nc.vector.tensor_copy(sg0[:], xs[:].bitcast(U8).indirect(list_cols(0, GATHER)))
-        nc.vector.tensor_copy(sg1[:], xs[:].bitcast(U8).indirect(list_cols(GATHER, GATHER)))
-        nc.vector.tensor_copy(sg23[:], xs[:].bitcast(U8).indirect(list_cols(2 * GATHER, 2 * GATHER)))
-        sg = {0: sg0[:], 1: sg1[:], 2: sg23[:, 0:GATHER], 3: sg23[:, GATHER:]}
+        permute(0, w1_a[:])
+        sg = keep.tile([P, E * C], U8, name="sg", align_bytes=64)
+        for half in range(2):
+            nc.vector.tensor_copy(
+                sg[:, half * 2 * PAIR : (half + 1) * 2 * PAIR],
+                xs[:].bitcast(U8).indirect(list_cols(half * 2 * PAIR, 2 * PAIR)),
+            )
 
-        xg01 = keep.tile([P, 2 * GATHER], U32, name="xg01", tag="slot_a", align_bytes=64)
-        xg = {0: xg01[:, 0:GATHER], 1: xg01[:, GATHER:]}
+        xg = {}
 
-        def gather(c):
-            if c == 2:
-                xg[c] = keep.tile([P, GATHER], U32, name="xg2", tag="slot_b", align_bytes=64)[:]
-            if c == 3:
-                xg[c] = keep.tile([P, GATHER], U32, name="xg3", tag="slot_c", align_bytes=64)[:]
-            nc.vector.tensor_copy(xg[c], xw[:].bitcast(U32).indirect(list_cols(c * GATHER, GATHER)))
+        def gather(pair):
+            if pair % 2 == 0:
+                tag = "slot_a" if pair == 0 else "slot_b"
+                both = keep.tile([P, 2, PAIR], U32, name="xg%d" % pair, tag=tag, align_bytes=64)
+                xg[pair] = both[:, 0, :]
+                xg[pair + 1] = both[:, 1, :]
+            nc.vector.tensor_copy(xg[pair], xw[:].bitcast(U32).indirect(list_cols(pair * PAIR, PAIR)))
 
         out_v = out.rearrange("(g p) (m c) -> g p m c", p=P, m=RANKS)
         hidden = {}
 
         def layer1(e):
-            c = e * C // GATHER
             h = work.tile([P, C, PACK], BF16, name="h", align_bytes=64)
             for m in range(RANKS):
-                c0 = (e * C) % GATHER + m * U
+                c0 = (e % 2) * C + m * U
                 a = psum_a.tile([P, PACK, U], F32, name="a")
                 for t in range(PACK):
                     nc.tensor.matmul_mx(
                         out=a[:, t, :],
-                        lhsT=w1p[e][:, t * P // 2 : (t + 1) * P // 2].bitcast(FP4X4),
-                        lhsT_scale=planes[:, e, t * P // 4 : (t + 1) * P // 4].bitcast(U8),
-                        rhs=xg[c][:, c0 : c0 + U].bitcast(FP8X4),
-                        rhs_scale=sg[c][:, c0 : c0 + U],
+                        lhsT=w1p[e // 2][:, e % 2, t * P // 2 : (t + 1) * P // 2].bitcast(FP4X4),
+                        lhsT_scale=s1[:, e, t * P // 4 : (t + 1) * P // 4].bitcast(U8),
+                        rhs=xg[e // 2][:, c0 : c0 + U].bitcast(FP8X4),
+                        rhs_scale=sg[:, e * C + m * U : e * C + (m + 1) * U],
                         start=True,
                         stop=True,
                     )
@@ -130,7 +128,7 @@ def tile_moe_pke_mlp_silu_kernel(tc, x_words, x_scales, w1_words, w1_scales, w2_
             nc.tensor.matmul_mx(
                 out=y,
                 lhsT=w2[:, e, g * P // 2 : (g + 1) * P // 2].bitcast(FP4X4),
-                lhsT_scale=planes[:, e, (H + g * P) // 4 : (H + (g + 1) * P) // 4].bitcast(U8),
+                lhsT_scale=s2[:, e, g * P // 4 : (g + 1) * P // 4].bitcast(U8),
                 rhs=hq.bitcast(FP8X4),
                 rhs_scale=hs,
                 start=True,
@@ -143,51 +141,63 @@ def tile_moe_pke_mlp_silu_kernel(tc, x_words, x_scales, w1_words, w1_scales, w2_
             nc.vector.quantize_mx(out=hq[:].bitcast(FP8X4), scales=hs[:], in_=values.rearrange("p c t -> p (c t)"))
             return hq[:], hs[:]
 
+        staged = {}
+
         def layer2(e):
             hq, hs = quantise(hidden[e][:], C)
-            y = psum_y.tile([P, N // P, C], F32, name="y")
-            for g in range(N // P):
+            y = psum_y.tile([P, G, C], F32, name="y")
+            for g in range(G):
                 product2(e, g, hq, hs, y[:, g, :])
-            staged = work.tile([P, N // P, C], F32, name="staged")
+            first = e - e % 2
+            count = 2 if e < E - 2 else 1
+            if e == first:
+                staged[first] = keep.tile([P, G, RANKS, count * U], F32, name="staged%d" % e)
+            dst = staged[first][:, :, :, (e - first) * U : (e - first + 1) * U]
+            src = y[:].rearrange("p g (m u) -> p g m u", m=RANKS)
             if e < SCALAR_COPIES:
-                nc.scalar.copy(staged[:], y[:])
+                nc.scalar.copy(dst, src)
             else:
-                nc.vector.tensor_copy(staged[:], y[:])
-            for g in range(N // P):
-                nc.sync.dma_start(
-                    out_v[g, :, :, e * U : (e + 1) * U],
-                    staged[:, g, :].rearrange("p (m u) -> p m u", m=RANKS),
-                )
+                nc.vector.tensor_copy(dst, src)
+            if e == first + count - 1:
+                for g in range(G):
+                    nc.sync.dma_start(out_v[g, :, :, first * U : (first + count) * U], staged[first][:, g, :, :])
 
         def layer2_last(e):
-            for m in range(RANKS):
-                hq, hs = quantise(hidden[e][:, m * U : (m + 1) * U, :], U)
-                if m == 0:
-                    y = psum_y.tile([P, N // P, U], F32, name="y")
-                    staged = work.tile([P, N // P, U], F32, name="staged")
-                    for g in range(N // P):
-                        product2(e, g, hq, hs, y[:, g, :])
-                    nc.vector.tensor_copy(staged[:], y[:])
-                    nc.sync.dma_start(out_v[:, :, m, e * U : (e + 1) * U].rearrange("g p u -> p g u"), staged[:])
+            cols = slice(e * U, (e + 1) * U)
+            hq, hs = quantise(hidden[e][:, 0:U, :], U)
+            y = psum_y.tile([P, G, U], F32, name="y")
+            early = keep.tile([P, G, U], F32, name="early")
+            for g in range(G):
+                product2(e, g, hq, hs, y[:, g, :])
+            nc.vector.tensor_copy(early[:], y[:])
+            nc.sync.dma_start(out_v[:, :, 0, cols].rearrange("g p u -> p g u"), early[:])
+            hq, hs = quantise(hidden[e][:, U:C, :], U)
+            for g in range(G):
+                y = psum_y.tile([P, U], F32, name="y")
+                last = keep.tile([P, U], F32, name="last%d" % g)
+                product2(e, g, hq, hs, y[:])
+                if g == 0:
+                    nc.vector.tensor_copy(last[:], y[:])
+                    nc.sync.dma_start(out_v[g, :, 1, cols], last[:])
                 else:
-                    for g in range(N // P):
-                        y = psum_y.tile([P, U], F32, name="y")
-                        staged = work.tile([P, U], F32, name="staged")
-                        product2(e, g, hq, hs, y[:])
-                        if g == 0:
-                            nc.vector.tensor_copy(staged[:], y[:])
-                            nc.sync.dma_start(out_v[g, :, m, e * U : (e + 1) * U], staged[:])
-                        else:
-                            nc.scalar.copy(staged[:], y[:])
-                            nc.scalar.dma_start(out_v[g, :, m, e * U : (e + 1) * U], staged[:])
+                    nc.scalar.copy(last[:], y[:])
+                    nc.scalar.dma_start(out_v[g, :, 1, cols], last[:])
 
         gather(0)
-        for e in range(E):
+        gather(1)
+        permute(1, w1_b[:])
+        layer1(0)
+        layer1(1)
+        gather(2)
+        layer2(0)
+        layer1(2)
+        gather(3)
+        layer2(1)
+        permute(2, w1_c[:, 0:2, :])
+        layer1(3)
+        layer2(2)
+        permute(3, w1_c[:, 2:4, :])
+        for e in range(4, E):
             layer1(e)
-            if e % 2 == 0 and e + 2 < E:
-                gather(e // 2 + 1)
-            if e + EARLY < E:
-                permute(e + EARLY, w1_late[:, e, :])
-            if e >= 1:
-                layer2(e - 1)
+            layer2(e - 1)
         layer2_last(E - 1)

@@ -14,12 +14,16 @@ SILU = mybir.ActivationFunctionType.Silu
 
 P = 128
 PACK = 4
+QUAD = 32
+ROWS = 4
 K, T, E, C, H, N = 512, 4096, 8, 256, 512, 256
 RANKS = 2
 U = C // RANKS
 G = N // P
 PAIR = 2 * C
-SCALAR_COPIES = 4
+HALF = E * C // 2
+LINE = 8
+VECTOR_ONLY = (1, 2, 3)
 FLOPS = 2 * E * C * (K * H + H * N)
 
 
@@ -28,176 +32,208 @@ def tile_moe_pke_mlp_silu_kernel(tc, x_words, x_scales, w1_words, w1_scales, w2_
     with ExitStack() as ctx:
         keep = ctx.enter_context(tc.tile_pool(name="keep", bufs=1))
         work = ctx.enter_context(tc.tile_pool(name="work", bufs=4))
-        psum_a = ctx.enter_context(tc.psum_pool(name="psum_a", bufs=4))
-        psum_y = ctx.enter_context(tc.psum_pool(name="psum_y", bufs=4))
+        psum_a = ctx.enter_context(tc.psum_pool(name="psum_a", bufs=5))
+        psum_y = ctx.enter_context(tc.psum_pool(name="psum_y", bufs=3))
 
         offsets = keep.tile([P, E * C // 16], U16, name="offsets")
-        xw = keep.tile([P, T], I32, name="xw", align_bytes=64)
-        xs = keep.tile([P, T // 4], I32, name="xs", tag="slot_a", align_bytes=64)
+        x_all = keep.tile([P, T], I32, name="x_all", align_bytes=64)
+        x_rows = keep.tile([P, T // 4], I32, name="x_rows", tag="rows_then_words", align_bytes=64)
         s1_raw = keep.tile([P, H // 4], I32, name="s1_raw", align_bytes=64)
-        s1_mid = keep.tile([P, H // 4], I32, name="s1_mid", align_bytes=64)
-        s1 = keep.tile([P, E, H // 4], I32, name="s1", align_bytes=64)
-        s2 = keep.tile([P, E, N // 4], I32, name="s2", align_bytes=64)
-        w1_a = keep.tile([P, 2, H // 2], I32, name="w1_a", align_bytes=64)
-        w1_b = keep.tile([P, 2, H // 2], I32, name="w1_b", tag="slot_b", align_bytes=64)
-        w1_c = keep.tile([P, 4, H // 2], I32, name="w1_c", align_bytes=64)
+        s1_turned = keep.tile([P, H // 4], I32, name="s1_turned", align_bytes=64)
+        s1_plane = keep.tile([P, E, H // 4], I32, name="s1_plane", align_bytes=64)
+        s2_plane = keep.tile([P, E, N // 4], I32, name="s2_plane", align_bytes=64)
+        w1_raw = [
+            keep.tile([P, 2, H // 2], I32, name="w1_raw%d" % pair, tag="w1_raw%d" % pair, align_bytes=64)
+            for pair in range(E // 2)
+        ]
         w2 = keep.tile([P, E, N // 2], I32, name="w2", align_bytes=64)
+        x_plane = keep.tile([P, E * C // 4], I32, name="x_plane", align_bytes=64)
         warm_in = keep.tile([P, 1], F32, name="warm_in")
         warm_out = keep.tile([P, 1], F32, name="warm_out")
 
-        nc.vector.memset(xs[:], 0)
+        nc.vector.memset(x_rows[:], 0)
         nc.vector.memset(warm_in[:], 0.0)
-        nc.vector.memset(s1[:], 0)
-        nc.vector.memset(s2[:], 0)
+        nc.vector.memset(s1_plane[:], 0)
+        nc.vector.memset(s2_plane[:], 0)
+        nc.vector.memset(x_plane[:], 0)
 
         w1_hbm = w1_words.rearrange("e s p b -> p (e s) b").bitcast(I32)
         w2_hbm = w2_words.rearrange("e s p b -> p (e s) b").bitcast(I32)
         s2_hbm = w2_scales.rearrange("e s q i -> q (e s) i").bitcast(I32)
+
+        def load_w1(pair):
+            nc.sync.dma_start(w1_raw[pair][:], w1_hbm[:, 2 * pair : 2 * pair + 2, :])
+
         nc.sync.dma_start(offsets[:], offs)
-        nc.sync.dma_start(s1_raw[:], w1_scales.rearrange("e s q i -> q (e s) i").bitcast(I32))
-        nc.sync.dma_start(w1_a[:], w1_hbm[:, 0:2, :])
-        for r in range(4):
-            nc.sync.dma_start(xs[r:P:32, :], x_scales[0, r:16:4, :].bitcast(I32))
-        nc.sync.dma_start(xw[:], x_words[0].rearrange("p t r -> p (t r)").bitcast(I32))
+        for q in range(P // QUAD):
+            nc.sync.dma_start(
+                s1_raw[QUAD * q : QUAD * (q + 1), :], w1_scales[:, 0, ROWS * q : ROWS * (q + 1), :].bitcast(I32)
+            )
+        nc.sync.dma_start(x_rows[0:P:8, :], x_scales[0].bitcast(I32))
+        load_w1(0)
+        nc.sync.dma_start(x_all[:], x_words[0].rearrange("p t r -> p (t r)").bitcast(I32))
         nc.scalar.activation(warm_out[:], warm_in[:], SILU)
 
         nc.vector.tensor_copy(
-            s1_mid[:].bitcast(U8).rearrange("p (t m) -> p t m", t=PACK),
+            s1_turned[:].bitcast(U8).rearrange("p (t m) -> p t m", t=PACK),
             s1_raw[:].bitcast(U8).rearrange("p (m t) -> p t m", t=PACK),
         )
-        for q in (0, 2, 1, 3):
-            nc.sync.dma_start(s1[32 * q : 32 * q + 4, :, :], s1_mid[32 * q : 32 * q + 32, :])
-        nc.sync.dma_start(w1_b[:], w1_hbm[:, 2:4, :])
-        nc.sync.dma_start(w2[:], w2_hbm)
-        for r in range(4):
-            nc.sync.dma_start(s2[r:P:32, :, :], s2_hbm[r:16:4, :, :])
-        nc.sync.dma_start(w1_c[:], w1_hbm[:, 4:E, :])
 
-        w1p = {}
+        w1_turned = {}
 
-        def permute(pair, raw):
-            w1p[pair] = keep.tile([P, 2, H // 2], I32, name="w1p%d" % pair, align_bytes=64)
+        def permute(pair):
+            w1_turned[pair] = keep.tile([P, PACK, 2, P // 2], I32, name="w1_turned%d" % pair, align_bytes=64)
             nc.vector.tensor_copy(
-                w1p[pair][:].bitcast(U16).rearrange("p e (t m) -> p e t m", t=PACK),
-                raw.bitcast(U16).rearrange("p e (m t) -> p e t m", t=PACK),
+                w1_turned[pair][:].bitcast(U16).rearrange("p t e (a b) -> p (e a) t b", b=LINE),
+                w1_raw[pair][:].bitcast(U16).rearrange("p e (a b t) -> p (e a) t b", b=LINE, t=PACK),
             )
 
-        def list_cols(first, count):
+        def list_piece(first, count):
             return offsets[:, first // 16 : (first + count) // 16]
 
-        permute(0, w1_a[:])
-        sg = keep.tile([P, E * C], U8, name="sg", align_bytes=64)
+        permute(0)
+        slot_rows = keep.tile([P, E * C], U8, name="slot_rows", align_bytes=64)
         for half in range(2):
             nc.vector.tensor_copy(
-                sg[:, half * 2 * PAIR : (half + 1) * 2 * PAIR],
-                xs[:].bitcast(U8).indirect(list_cols(half * 2 * PAIR, 2 * PAIR)),
+                slot_rows[:, half * HALF : (half + 1) * HALF],
+                x_rows[:].bitcast(U8).indirect(list_piece(half * HALF, HALF)),
             )
 
-        xg = {}
+        def spread_slot_rows(half):
+            for r in range(ROWS):
+                nc.sync.dma_start(
+                    x_plane[r:P:QUAD, half * HALF // 4 : (half + 1) * HALF // 4],
+                    slot_rows[8 * r : P : QUAD, half * HALF : (half + 1) * HALF].bitcast(I32),
+                )
+
+        for r in range(ROWS):
+            nc.sync.dma_start(s2_plane[r:P:QUAD, :, :], s2_hbm[r : K // 32 : ROWS, :, :])
+        for r in range(ROWS):
+            nc.sync.dma_start(s1_plane[r:P:QUAD, :, :], s1_turned[r:P:ROWS, :])
+        spread_slot_rows(0)
+        load_w1(1)
+        spread_slot_rows(1)
+        load_w1(2)
+        nc.sync.dma_start(w2[:], w2_hbm)
+        load_w1(3)
+
+        first_words = keep.tile([P, 2, PAIR], U32, name="first_words", tag="rows_then_words", align_bytes=64)
+        slot_words = [
+            first_words[:, 0, :],
+            first_words[:, 1, :],
+            keep.tile([P, PAIR], U32, name="third_words", tag="w1_raw1", align_bytes=64)[:],
+            keep.tile([P, PAIR], U32, name="fourth_words", align_bytes=64)[:],
+        ]
 
         def gather(pair):
-            if pair % 2 == 0:
-                tag = "slot_a" if pair == 0 else "slot_b"
-                both = keep.tile([P, 2, PAIR], U32, name="xg%d" % pair, tag=tag, align_bytes=64)
-                xg[pair] = both[:, 0, :]
-                xg[pair + 1] = both[:, 1, :]
-            nc.vector.tensor_copy(xg[pair], xw[:].bitcast(U32).indirect(list_cols(pair * PAIR, PAIR)))
+            nc.vector.tensor_copy(slot_words[pair], x_all[:].bitcast(U32).indirect(list_piece(pair * PAIR, PAIR)))
 
-        out_v = out.rearrange("(g p) (m c) -> g p m c", p=P, m=RANKS)
+        out_blocks = out.rearrange("(g p) (m c) -> g p m c", p=P, m=RANKS)
         hidden = {}
 
         def layer1(e):
-            h = work.tile([P, C, PACK], BF16, name="h", align_bytes=64)
+            h = work.tile([P, C, PACK], BF16, name="h", bufs=3, align_bytes=64)
             for m in range(RANKS):
-                c0 = (e % 2) * C + m * U
+                in_pair = (e % 2) * C + m * U
+                slot = e * C + m * U
                 a = psum_a.tile([P, PACK, U], F32, name="a")
                 for t in range(PACK):
                     nc.tensor.matmul_mx(
                         out=a[:, t, :],
-                        lhsT=w1p[e // 2][:, e % 2, t * P // 2 : (t + 1) * P // 2].bitcast(FP4X4),
-                        lhsT_scale=s1[:, e, t * P // 4 : (t + 1) * P // 4].bitcast(U8),
-                        rhs=xg[e // 2][:, c0 : c0 + U].bitcast(FP8X4),
-                        rhs_scale=sg[:, e * C + m * U : e * C + (m + 1) * U],
+                        lhsT=w1_turned[e // 2][:, t, e % 2, :].bitcast(FP4X4),
+                        lhsT_scale=s1_plane[:, e, t * P // 4 : (t + 1) * P // 4].bitcast(U8),
+                        rhs=slot_words[e // 2][:, in_pair : in_pair + U].bitcast(FP8X4),
+                        rhs_scale=x_plane[:, slot // 4 : (slot + U) // 4].bitcast(U8),
                         start=True,
                         stop=True,
                     )
                 nc.scalar.activation(h[:, m * U : (m + 1) * U, :], a[:].rearrange("p t u -> p u t"), SILU)
             hidden[e] = h
 
-        def product2(e, g, hq, hs, y):
+        def quantise(values, width, after_last_permute=False):
+            if after_last_permute:
+                h_words = keep.tile([P, width], U32, name="h_words_late", tag="w1_raw3", align_bytes=64)
+            else:
+                h_words = work.tile([P, width], U32, name="h_words", align_bytes=64)
+            h_plane = work.tile([P, width], U8, name="h_plane", align_bytes=64)
+            nc.vector.quantize_mx(
+                out=h_words[:].bitcast(FP8X4), scales=h_plane[:], in_=values.rearrange("p c t -> p (c t)")
+            )
+            return h_words[:], h_plane[:]
+
+        def product2(e, g, h_words, h_plane, y):
             nc.tensor.matmul_mx(
                 out=y,
                 lhsT=w2[:, e, g * P // 2 : (g + 1) * P // 2].bitcast(FP4X4),
-                lhsT_scale=s2[:, e, g * P // 4 : (g + 1) * P // 4].bitcast(U8),
-                rhs=hq.bitcast(FP8X4),
-                rhs_scale=hs,
+                lhsT_scale=s2_plane[:, e, g * P // 4 : (g + 1) * P // 4].bitcast(U8),
+                rhs=h_words.bitcast(FP8X4),
+                rhs_scale=h_plane,
                 start=True,
                 stop=True,
             )
 
-        def quantise(values, width):
-            hq = work.tile([P, width], U32, name="hq", align_bytes=64)
-            hs = work.tile([P, width], U8, name="hs", align_bytes=64)
-            nc.vector.quantize_mx(out=hq[:].bitcast(FP8X4), scales=hs[:], in_=values.rearrange("p c t -> p (c t)"))
-            return hq[:], hs[:]
-
-        staged = {}
+        def copy_block(g, staged, y):
+            if g == 0:
+                nc.vector.tensor_copy(staged, y)
+            else:
+                nc.scalar.copy(staged, y)
 
         def layer2(e):
-            hq, hs = quantise(hidden[e][:], C)
-            y = psum_y.tile([P, G, C], F32, name="y")
-            for g in range(G):
-                product2(e, g, hq, hs, y[:, g, :])
-            first = e - e % 2
-            count = 2 if e < E - 2 else 1
-            if e == first:
-                staged[first] = keep.tile([P, G, RANKS, count * U], F32, name="staged%d" % e)
-            dst = staged[first][:, :, :, (e - first) * U : (e - first + 1) * U]
-            src = y[:].rearrange("p g (m u) -> p g m u", m=RANKS)
-            if e < SCALAR_COPIES:
-                nc.scalar.copy(dst, src)
-            else:
-                nc.vector.tensor_copy(dst, src)
-            if e == first + count - 1:
-                for g in range(G):
-                    nc.sync.dma_start(out_v[g, :, :, first * U : (first + count) * U], staged[first][:, g, :, :])
-
-        def layer2_last(e):
             cols = slice(e * U, (e + 1) * U)
-            hq, hs = quantise(hidden[e][:, 0:U, :], U)
+            h_words, h_plane = quantise(hidden[e][:], C, after_last_permute=e == E // 2)
+            if e in VECTOR_ONLY:
+                y = psum_y.tile([P, G, C], F32, name="y")
+                for g in range(G):
+                    product2(e, g, h_words, h_plane, y[:, g, :])
+                staged = keep.tile([P, G, RANKS, U], F32, name="staged%d" % e)
+                nc.vector.tensor_copy(staged[:], y[:].rearrange("p g (m u) -> p g m u", m=RANKS))
+                for g in range(G):
+                    nc.sync.dma_start(out_blocks[g, :, :, cols], staged[:, g, :, :])
+            else:
+                for g in range(G):
+                    y = psum_y.tile([P, C], F32, name="y")
+                    staged = keep.tile([P, C], F32, name="staged%d_%d" % (e, g))
+                    product2(e, g, h_words, h_plane, y[:])
+                    copy_block(g, staged[:], y[:])
+                    nc.sync.dma_start(out_blocks[g, :, :, cols], staged[:].rearrange("p (m u) -> p m u", m=RANKS))
+
+        def layer2_by_rank(e):
+            cols = slice(e * U, (e + 1) * U)
+            h_words, h_plane = quantise(hidden[e][:, 0:U, :], U)
             y = psum_y.tile([P, G, U], F32, name="y")
-            early = keep.tile([P, G, U], F32, name="early")
+            staged = keep.tile([P, G, U], F32, name="staged_rank0")
             for g in range(G):
-                product2(e, g, hq, hs, y[:, g, :])
-            nc.vector.tensor_copy(early[:], y[:])
-            nc.sync.dma_start(out_v[:, :, 0, cols].rearrange("g p u -> p g u"), early[:])
-            hq, hs = quantise(hidden[e][:, U:C, :], U)
-            for g in range(G):
+                product2(e, g, h_words, h_plane, y[:, g, :])
+            nc.scalar.copy(staged[:], y[:])
+            nc.sync.dma_start(out_blocks[:, :, 0, cols].rearrange("g p u -> p g u"), staged[:])
+            h_words, h_plane = quantise(hidden[e][:, U:C, :], U)
+            for g, queue in enumerate((nc.sync, nc.scalar)):
                 y = psum_y.tile([P, U], F32, name="y")
-                last = keep.tile([P, U], F32, name="last%d" % g)
-                product2(e, g, hq, hs, y[:])
-                if g == 0:
-                    nc.vector.tensor_copy(last[:], y[:])
-                    nc.sync.dma_start(out_v[g, :, 1, cols], last[:])
-                else:
-                    nc.scalar.copy(last[:], y[:])
-                    nc.scalar.dma_start(out_v[g, :, 1, cols], last[:])
+                staged = keep.tile([P, U], F32, name="staged_rank1_%d" % g)
+                product2(e, g, h_words, h_plane, y[:])
+                copy_block(g, staged[:], y[:])
+                queue.dma_start(out_blocks[g, :, 1, cols], staged[:])
 
         gather(0)
-        gather(1)
-        permute(1, w1_b[:])
-        layer1(0)
-        layer1(1)
         gather(2)
-        layer2(0)
+        layer1(0)
+        permute(3)
+        permute(1)
+        layer1(1)
+        gather(1)
         layer1(2)
-        gather(3)
-        layer2(1)
-        permute(2, w1_c[:, 0:2, :])
+        layer2(0)
         layer1(3)
+        layer2(1)
+        permute(2)
+        layer1(4)
+        layer1(5)
+        gather(3)
         layer2(2)
-        permute(3, w1_c[:, 2:4, :])
-        for e in range(4, E):
-            layer1(e)
-            layer2(e - 1)
-        layer2_last(E - 1)
+        layer1(6)
+        layer2(3)
+        layer2(4)
+        layer2(5)
+        layer1(7)
+        layer2(6)
+        layer2_by_rank(7)

@@ -22,8 +22,13 @@ U = C // RANKS
 G = N // P
 PAIR = 2 * C
 HALF = E * C // 2
+X_FIRST = 3 * T // 4
 LINE = 8
-VECTOR_ONLY = (1, 2, 3)
+SCALAR_ONLY = (0, 6)
+FIRST_BANKS = (0, 1, 2, 3, 4, 5, 6, 7)
+LATER_BANKS = (0, 1, 2, 4, 3, 6, 2, 5)
+Y_BANK = (3, 5, 0, 1, 4, 6, 7)
+LAST_BANKS = (0, 1, 4)
 FLOPS = 2 * E * C * (K * H + H * N)
 
 
@@ -31,31 +36,30 @@ def tile_moe_pke_mlp_silu_kernel(tc, x_words, x_scales, w1_words, w1_scales, w2_
     nc = tc.nc
     with ExitStack() as ctx:
         keep = ctx.enter_context(tc.tile_pool(name="keep", bufs=1))
-        work = ctx.enter_context(tc.tile_pool(name="work", bufs=4))
-        psum_a = ctx.enter_context(tc.psum_pool(name="psum_a", bufs=5))
-        psum_y = ctx.enter_context(tc.psum_pool(name="psum_y", bufs=3))
+        psum = ctx.enter_context(tc.psum_pool(name="psum", bufs=1))
+
+        def bank(number, shape, name):
+            return psum.tile(shape, F32, name=name, tag="bank%d" % number)
 
         offsets = keep.tile([P, E * C // 16], U16, name="offsets")
         x_all = keep.tile([P, T], I32, name="x_all", align_bytes=64)
-        x_rows = keep.tile([P, T // 4], I32, name="x_rows", tag="rows_then_words", align_bytes=64)
-        s1_raw = keep.tile([P, H // 4], I32, name="s1_raw", align_bytes=64)
+        x_rows = keep.tile([P, T // 4], I32, name="x_rows", tag="x_rows", align_bytes=64)
+        s1_raw = keep.tile([P, H // 4], I32, name="s1_raw", tag="s1_raw", align_bytes=64)
         s1_turned = keep.tile([P, H // 4], I32, name="s1_turned", align_bytes=64)
         s1_plane = keep.tile([P, E, H // 4], I32, name="s1_plane", align_bytes=64)
-        s2_plane = keep.tile([P, E, N // 4], I32, name="s2_plane", align_bytes=64)
         w1_raw = [
             keep.tile([P, 2, H // 2], I32, name="w1_raw%d" % pair, tag="w1_raw%d" % pair, align_bytes=64)
             for pair in range(E // 2)
         ]
-        w2 = keep.tile([P, E, N // 2], I32, name="w2", align_bytes=64)
+        w2 = [keep.tile([P, E // 2, N // 2], I32, name="w2_%d" % half, align_bytes=64) for half in range(2)]
         x_plane = keep.tile([P, E * C // 4], I32, name="x_plane", align_bytes=64)
         warm_in = keep.tile([P, 1], F32, name="warm_in")
         warm_out = keep.tile([P, 1], F32, name="warm_out")
 
         nc.vector.memset(x_rows[:], 0)
-        nc.vector.memset(warm_in[:], 0.0)
         nc.vector.memset(s1_plane[:], 0)
-        nc.vector.memset(s2_plane[:], 0)
         nc.vector.memset(x_plane[:], 0)
+        nc.vector.memset(warm_in[:], 0.0)
 
         w1_hbm = w1_words.rearrange("e s p b -> p (e s) b").bitcast(I32)
         w2_hbm = w2_words.rearrange("e s p b -> p (e s) b").bitcast(I32)
@@ -65,13 +69,14 @@ def tile_moe_pke_mlp_silu_kernel(tc, x_words, x_scales, w1_words, w1_scales, w2_
             nc.sync.dma_start(w1_raw[pair][:], w1_hbm[:, 2 * pair : 2 * pair + 2, :])
 
         nc.sync.dma_start(offsets[:], offs)
-        for q in range(P // QUAD):
-            nc.sync.dma_start(
+        for q, queue in enumerate((nc.sync, nc.sync, nc.scalar, nc.scalar)):
+            queue.dma_start(
                 s1_raw[QUAD * q : QUAD * (q + 1), :], w1_scales[:, 0, ROWS * q : ROWS * (q + 1), :].bitcast(I32)
             )
-        nc.sync.dma_start(x_rows[0:P:8, :], x_scales[0].bitcast(I32))
         load_w1(0)
-        nc.sync.dma_start(x_all[:], x_words[0].rearrange("p t r -> p (t r)").bitcast(I32))
+        nc.sync.dma_start(x_rows[0:P:8, :], x_scales[0].bitcast(I32))
+        x_hbm = x_words[0].rearrange("p t r -> p (t r)").bitcast(I32)
+        nc.sync.dma_start(x_all[:, 0:X_FIRST], x_hbm[:, 0:X_FIRST])
         nc.scalar.activation(warm_out[:], warm_in[:], SILU)
 
         nc.vector.tensor_copy(
@@ -91,52 +96,53 @@ def tile_moe_pke_mlp_silu_kernel(tc, x_words, x_scales, w1_words, w1_scales, w2_
         def list_piece(first, count):
             return offsets[:, first // 16 : (first + count) // 16]
 
-        permute(0)
-        slot_rows = keep.tile([P, E * C], U8, name="slot_rows", align_bytes=64)
-        for half in range(2):
-            nc.vector.tensor_copy(
-                slot_rows[:, half * HALF : (half + 1) * HALF],
-                x_rows[:].bitcast(U8).indirect(list_piece(half * HALF, HALF)),
-            )
+        def gather_rows(first, count, name, tag):
+            rows = keep.tile([P, count], U8, name=name, tag=tag, align_bytes=64)
+            nc.vector.tensor_copy(rows[:], x_rows[:].bitcast(U8).indirect(list_piece(first, count)))
+            return rows
 
-        def spread_slot_rows(half):
+        def spread_rows(rows, first, count):
             for r in range(ROWS):
                 nc.sync.dma_start(
-                    x_plane[r:P:QUAD, half * HALF // 4 : (half + 1) * HALF // 4],
-                    slot_rows[8 * r : P : QUAD, half * HALF : (half + 1) * HALF].bitcast(I32),
+                    x_plane[r:P:QUAD, first // 4 : (first + count) // 4],
+                    rows[8 * r : P : QUAD, :].bitcast(I32),
                 )
 
-        for r in range(ROWS):
-            nc.sync.dma_start(s2_plane[r:P:QUAD, :, :], s2_hbm[r : K // 32 : ROWS, :, :])
+        permute(0)
+        rows_first = gather_rows(0, HALF, "rows_first", "rows_first")
+        rows_second = gather_rows(HALF, HALF, "rows_second", "rows_second")
         for r in range(ROWS):
             nc.sync.dma_start(s1_plane[r:P:QUAD, :, :], s1_turned[r:P:ROWS, :])
-        spread_slot_rows(0)
+            if r == 0:
+                nc.sync.dma_start(x_all[:, X_FIRST:T], x_hbm[:, X_FIRST:T])
+        spread_rows(rows_first, 0, HALF)
         load_w1(1)
-        spread_slot_rows(1)
         load_w1(2)
-        nc.sync.dma_start(w2[:], w2_hbm)
+        s2_plane = w1_raw[0][:].rearrange("p a (b c) -> p (a b) c", c=N // 4)
+        for r in range(ROWS):
+            nc.sync.dma_start(s2_plane[r:P:QUAD, :, :], s2_hbm[r : K // 32 : ROWS, :, :])
+        nc.sync.dma_start(w2[0][:], w2_hbm[:, 0 : E // 2, :])
         load_w1(3)
+        spread_rows(rows_second, HALF, HALF)
+        nc.sync.dma_start(w2[1][:], w2_hbm[:, E // 2 : E, :])
 
-        first_words = keep.tile([P, 2, PAIR], U32, name="first_words", tag="rows_then_words", align_bytes=64)
-        slot_words = [
-            first_words[:, 0, :],
-            first_words[:, 1, :],
-            keep.tile([P, PAIR], U32, name="third_words", tag="w1_raw1", align_bytes=64)[:],
-            keep.tile([P, PAIR], U32, name="fourth_words", align_bytes=64)[:],
-        ]
+        slot_words = {}
 
-        def gather(pair):
-            nc.vector.tensor_copy(slot_words[pair], x_all[:].bitcast(U32).indirect(list_piece(pair * PAIR, PAIR)))
+        def gather(pair, tag):
+            words = keep.tile([P, PAIR], U32, name="words%d" % pair, tag=tag, align_bytes=64)
+            nc.vector.tensor_copy(words[:], x_all[:].bitcast(U32).indirect(list_piece(pair * PAIR, PAIR)))
+            slot_words[pair] = words
 
         out_blocks = out.rearrange("(g p) (m c) -> g p m c", p=P, m=RANKS)
         hidden = {}
+        codes = {}
 
         def layer1(e):
-            h = work.tile([P, C, PACK], BF16, name="h", bufs=3, align_bytes=64)
+            h = keep.tile([P, C, PACK], BF16, name="h%d" % e, tag="h%d" % e, align_bytes=64)
             for m in range(RANKS):
                 in_pair = (e % 2) * C + m * U
                 slot = e * C + m * U
-                a = psum_a.tile([P, PACK, U], F32, name="a")
+                a = bank((FIRST_BANKS + LATER_BANKS)[RANKS * e + m], [P, PACK, U], "a")
                 for t in range(PACK):
                     nc.tensor.matmul_mx(
                         out=a[:, t, :],
@@ -150,12 +156,9 @@ def tile_moe_pke_mlp_silu_kernel(tc, x_words, x_scales, w1_words, w1_scales, w2_
                 nc.scalar.activation(h[:, m * U : (m + 1) * U, :], a[:].rearrange("p t u -> p u t"), SILU)
             hidden[e] = h
 
-        def quantise(values, width, after_last_permute=False):
-            if after_last_permute:
-                h_words = keep.tile([P, width], U32, name="h_words_late", tag="w1_raw3", align_bytes=64)
-            else:
-                h_words = work.tile([P, width], U32, name="h_words", align_bytes=64)
-            h_plane = work.tile([P, width], U8, name="h_plane", align_bytes=64)
+        def quantise(values, width, name):
+            h_words = keep.tile([P, width], U32, name=name, tag=name, align_bytes=64)
+            h_plane = keep.tile([P, width], U8, name=name + "_plane", align_bytes=64)
             nc.vector.quantize_mx(
                 out=h_words[:].bitcast(FP8X4), scales=h_plane[:], in_=values.rearrange("p c t -> p (c t)")
             )
@@ -164,7 +167,7 @@ def tile_moe_pke_mlp_silu_kernel(tc, x_words, x_scales, w1_words, w1_scales, w2_
         def product2(e, g, h_words, h_plane, y):
             nc.tensor.matmul_mx(
                 out=y,
-                lhsT=w2[:, e, g * P // 2 : (g + 1) * P // 2].bitcast(FP4X4),
+                lhsT=w2[e // (E // 2)][:, e % (E // 2), g * P // 2 : (g + 1) * P // 2].bitcast(FP4X4),
                 lhsT_scale=s2_plane[:, e, g * P // 4 : (g + 1) * P // 4].bitcast(U8),
                 rhs=h_words.bitcast(FP8X4),
                 rhs_scale=h_plane,
@@ -172,67 +175,69 @@ def tile_moe_pke_mlp_silu_kernel(tc, x_words, x_scales, w1_words, w1_scales, w2_
                 stop=True,
             )
 
-        def copy_block(g, staged, y):
-            if g == 0:
-                nc.vector.tensor_copy(staged, y)
-            else:
+        def copy_out(on_scalar, staged, y):
+            if on_scalar:
                 nc.scalar.copy(staged, y)
+            else:
+                nc.vector.tensor_copy(staged, y)
+
+        def quantise_expert(e):
+            codes[e] = quantise(hidden[e][:], C, "h_words%d" % e)
 
         def layer2(e):
             cols = slice(e * U, (e + 1) * U)
-            h_words, h_plane = quantise(hidden[e][:], C, after_last_permute=e == E // 2)
-            if e in VECTOR_ONLY:
-                y = psum_y.tile([P, G, C], F32, name="y")
-                for g in range(G):
-                    product2(e, g, h_words, h_plane, y[:, g, :])
-                staged = keep.tile([P, G, RANKS, U], F32, name="staged%d" % e)
-                nc.vector.tensor_copy(staged[:], y[:].rearrange("p g (m u) -> p g m u", m=RANKS))
-                for g in range(G):
-                    nc.sync.dma_start(out_blocks[g, :, :, cols], staged[:, g, :, :])
-            else:
-                for g in range(G):
-                    y = psum_y.tile([P, C], F32, name="y")
-                    staged = keep.tile([P, C], F32, name="staged%d_%d" % (e, g))
-                    product2(e, g, h_words, h_plane, y[:])
-                    copy_block(g, staged[:], y[:])
-                    nc.sync.dma_start(out_blocks[g, :, :, cols], staged[:].rearrange("p (m u) -> p m u", m=RANKS))
+            h_words, h_plane = codes[e]
+            y = bank(Y_BANK[e], [P, G, C], "y")
+            for g in range(G):
+                product2(e, g, h_words, h_plane, y[:, g, :])
+            staged = keep.tile([P, G, RANKS, U], F32, name="staged%d" % e)
+            copy_out(e in SCALAR_ONLY, staged[:], y[:].rearrange("p g (m u) -> p g m u", m=RANKS))
+            for g in range(G):
+                nc.sync.dma_start(out_blocks[g, :, :, cols], staged[:, g, :, :])
 
         def layer2_by_rank(e):
             cols = slice(e * U, (e + 1) * U)
-            h_words, h_plane = quantise(hidden[e][:, 0:U, :], U)
-            y = psum_y.tile([P, G, U], F32, name="y")
+            h_words, h_plane = quantise(hidden[e][:, 0:U, :], U, "h_words_rank0")
+            y = bank(LAST_BANKS[0], [P, G, U], "y")
             staged = keep.tile([P, G, U], F32, name="staged_rank0")
             for g in range(G):
                 product2(e, g, h_words, h_plane, y[:, g, :])
-            nc.scalar.copy(staged[:], y[:])
+            nc.vector.tensor_copy(staged[:], y[:])
             nc.sync.dma_start(out_blocks[:, :, 0, cols].rearrange("g p u -> p g u"), staged[:])
-            h_words, h_plane = quantise(hidden[e][:, U:C, :], U)
+            h_words, h_plane = quantise(hidden[e][:, U:C, :], U, "h_words_rank1")
             for g, queue in enumerate((nc.sync, nc.scalar)):
-                y = psum_y.tile([P, U], F32, name="y")
+                y = bank(LAST_BANKS[1 + g], [P, U], "y")
                 staged = keep.tile([P, U], F32, name="staged_rank1_%d" % g)
                 product2(e, g, h_words, h_plane, y[:])
-                copy_block(g, staged[:], y[:])
+                copy_out(g == 1, staged[:], y[:])
                 queue.dma_start(out_blocks[g, :, 1, cols], staged[:])
 
-        gather(0)
-        gather(2)
-        layer1(0)
-        permute(3)
+        gather(0, "words0")
+        gather(1, "words1")
         permute(1)
+        layer1(0)
         layer1(1)
-        gather(1)
-        layer1(2)
-        layer2(0)
-        layer1(3)
-        layer2(1)
+        quantise_expert(0)
+        gather(2, "words0")
         permute(2)
+        layer1(2)
+        quantise_expert(1)
+        layer1(3)
+        gather(3, "words1")
+        quantise_expert(2)
+        quantise_expert(3)
+        layer2(0)
+        permute(3)
+        layer2(1)
         layer1(4)
-        layer1(5)
-        gather(3)
         layer2(2)
-        layer1(6)
+        quantise_expert(4)
         layer2(3)
+        layer1(5)
+        quantise_expert(5)
         layer2(4)
+        layer1(6)
+        quantise_expert(6)
         layer2(5)
         layer1(7)
         layer2(6)

@@ -22,13 +22,12 @@ U = C // RANKS
 G = N // P
 PAIR = 2 * C
 HALF = E * C // 2
-X_FIRST = 3 * T // 4
 LINE = 8
-SCALAR_ONLY = (0, 6)
-FIRST_BANKS = (0, 1, 2, 3, 4, 5, 6, 7)
-LATER_BANKS = (0, 1, 2, 4, 3, 6, 2, 5)
-Y_BANK = (3, 5, 0, 1, 4, 6, 7)
-LAST_BANKS = (0, 1, 4)
+SCALAR_ONLY = (1, 5, 6)
+A_ON_SCALAR = False
+A_BANK = (0, 1, 2, 3, 4, 5, 6, 7, 4, 5, 6, 7, 0, 1, 4, 5)
+Y_BANK = (0, 1, 2, 3, 6, 7, 0)
+LAST_BANKS = (1, 2, 3)
 FLOPS = 2 * E * C * (K * H + H * N)
 
 
@@ -41,63 +40,77 @@ def tile_moe_pke_mlp_silu_kernel(tc, x_words, x_scales, w1_words, w1_scales, w2_
         def bank(number, shape, name):
             return psum.tile(shape, F32, name=name, tag="bank%d" % number)
 
+        def sbuf(shape, dtype, name, tag=None):
+            return keep.tile(shape, dtype, name=name, tag=tag or name, align_bytes=64)
+
         offsets = keep.tile([P, E * C // 16], U16, name="offsets")
-        x_all = keep.tile([P, T], I32, name="x_all", align_bytes=64)
-        x_rows = keep.tile([P, T // 4], I32, name="x_rows", tag="x_rows", align_bytes=64)
-        s1_raw = keep.tile([P, H // 4], I32, name="s1_raw", tag="s1_raw", align_bytes=64)
-        s1_turned = keep.tile([P, H // 4], I32, name="s1_turned", align_bytes=64)
-        s1_plane = keep.tile([P, E, H // 4], I32, name="s1_plane", align_bytes=64)
-        w1_raw = [
-            keep.tile([P, 2, H // 2], I32, name="w1_raw%d" % pair, tag="w1_raw%d" % pair, align_bytes=64)
-            for pair in range(E // 2)
-        ]
-        w2 = [keep.tile([P, E // 2, N // 2], I32, name="w2_%d" % half, align_bytes=64) for half in range(2)]
-        x_plane = keep.tile([P, E * C // 4], I32, name="x_plane", align_bytes=64)
+        x_all = sbuf([P, T], I32, "x_all")
+        x_rows = sbuf([P, T // 4], I32, "x_rows")
+        s1_raw = sbuf([P, H // 4], I32, "s1_raw")
+        s1_turned = sbuf([P, H // 4], I32, "s1_turned")
+        s1_plane = sbuf([P, E, H // 4], I32, "s1_plane")
+        w1_raw = [sbuf([P, 2, H // 2], I32, "w1_raw%d" % pair) for pair in range(E // 2)]
+        w2 = [sbuf([P, E // 2, N // 2], I32, "w2_%d" % half) for half in range(2)]
+        x_plane = sbuf([P, E * C // 4], I32, "x_plane")
         warm_in = keep.tile([P, 1], F32, name="warm_in")
         warm_out = keep.tile([P, 1], F32, name="warm_out")
 
-        nc.vector.memset(x_rows[:], 0)
-        nc.vector.memset(s1_plane[:], 0)
-        nc.vector.memset(x_plane[:], 0)
-        nc.vector.memset(warm_in[:], 0.0)
-
+        x_hbm = x_words[0].rearrange("p t r -> p (t r)").bitcast(I32)
         w1_hbm = w1_words.rearrange("e s p b -> p (e s) b").bitcast(I32)
         w2_hbm = w2_words.rearrange("e s p b -> p (e s) b").bitcast(I32)
         s2_hbm = w2_scales.rearrange("e s q i -> q (e s) i").bitcast(I32)
+        out_blocks = out.rearrange("(g p) (m c) -> g p m c", p=P, m=RANKS)
+        s2_plane = w1_raw[0][:].rearrange("p a (b c) -> p (a b) c", c=N // 4)
+        w1_turned = {}
+        slot_words = {}
+        hidden = {}
+        codes = {}
+        sums = {}
+        done = []
+
+        def load_tokens(first, last):
+            nc.sync.dma_start(x_all[:, first:last], x_hbm[:, first:last])
 
         def load_w1(pair):
             nc.sync.dma_start(w1_raw[pair][:], w1_hbm[:, 2 * pair : 2 * pair + 2, :])
 
-        nc.sync.dma_start(offsets[:], offs)
-        for q, queue in enumerate((nc.sync, nc.sync, nc.scalar, nc.scalar)):
+        def load_w2(half):
+            nc.sync.dma_start(w2[half][:], w2_hbm[:, half * E // 2 : (half + 1) * E // 2, :])
+
+        def load_s1(q, queue):
             queue.dma_start(
                 s1_raw[QUAD * q : QUAD * (q + 1), :], w1_scales[:, 0, ROWS * q : ROWS * (q + 1), :].bitcast(I32)
             )
-        load_w1(0)
-        nc.sync.dma_start(x_rows[0:P:8, :], x_scales[0].bitcast(I32))
-        x_hbm = x_words[0].rearrange("p t r -> p (t r)").bitcast(I32)
-        nc.sync.dma_start(x_all[:, 0:X_FIRST], x_hbm[:, 0:X_FIRST])
-        nc.scalar.activation(warm_out[:], warm_in[:], SILU)
 
-        nc.vector.tensor_copy(
-            s1_turned[:].bitcast(U8).rearrange("p (t m) -> p t m", t=PACK),
-            s1_raw[:].bitcast(U8).rearrange("p (m t) -> p t m", t=PACK),
-        )
+        def load_s2():
+            for r in range(ROWS):
+                nc.sync.dma_start(s2_plane[r:P:QUAD, :, :], s2_hbm[r : K // 32 : ROWS, :, :])
 
-        w1_turned = {}
+        def load_token_scales():
+            nc.sync.dma_start(x_rows[0:P:8, :], x_scales[0].bitcast(I32))
+
+        def permute_scales():
+            nc.vector.tensor_copy(
+                s1_turned[:].bitcast(U8).rearrange("p (t m) -> p t m", t=PACK),
+                s1_raw[:].bitcast(U8).rearrange("p (m t) -> p t m", t=PACK),
+            )
 
         def permute(pair):
-            w1_turned[pair] = keep.tile([P, PACK, 2, P // 2], I32, name="w1_turned%d" % pair, align_bytes=64)
+            w1_turned[pair] = sbuf([P, PACK, 2, P // 2], I32, "w1_turned%d" % pair)
             nc.vector.tensor_copy(
                 w1_turned[pair][:].bitcast(U16).rearrange("p t e (a b) -> p (e a) t b", b=LINE),
                 w1_raw[pair][:].bitcast(U16).rearrange("p e (a b t) -> p (e a) t b", b=LINE, t=PACK),
             )
 
+        def spread_s1():
+            for r in range(ROWS):
+                nc.sync.dma_start(s1_plane[r:P:QUAD, :, :], s1_turned[r:P:ROWS, :])
+
         def list_piece(first, count):
             return offsets[:, first // 16 : (first + count) // 16]
 
-        def gather_rows(first, count, name, tag):
-            rows = keep.tile([P, count], U8, name=name, tag=tag, align_bytes=64)
+        def gather_rows(first, count, name):
+            rows = sbuf([P, count], U8, name)
             nc.vector.tensor_copy(rows[:], x_rows[:].bitcast(U8).indirect(list_piece(first, count)))
             return rows
 
@@ -108,57 +121,39 @@ def tile_moe_pke_mlp_silu_kernel(tc, x_words, x_scales, w1_words, w1_scales, w2_
                     rows[8 * r : P : QUAD, :].bitcast(I32),
                 )
 
-        permute(0)
-        rows_first = gather_rows(0, HALF, "rows_first", "rows_first")
-        rows_second = gather_rows(HALF, HALF, "rows_second", "rows_second")
-        for r in range(ROWS):
-            nc.sync.dma_start(s1_plane[r:P:QUAD, :, :], s1_turned[r:P:ROWS, :])
-            if r == 0:
-                nc.sync.dma_start(x_all[:, X_FIRST:T], x_hbm[:, X_FIRST:T])
-        spread_rows(rows_first, 0, HALF)
-        load_w1(1)
-        load_w1(2)
-        s2_plane = w1_raw[0][:].rearrange("p a (b c) -> p (a b) c", c=N // 4)
-        for r in range(ROWS):
-            nc.sync.dma_start(s2_plane[r:P:QUAD, :, :], s2_hbm[r : K // 32 : ROWS, :, :])
-        nc.sync.dma_start(w2[0][:], w2_hbm[:, 0 : E // 2, :])
-        load_w1(3)
-        spread_rows(rows_second, HALF, HALF)
-        nc.sync.dma_start(w2[1][:], w2_hbm[:, E // 2 : E, :])
-
-        slot_words = {}
-
         def gather(pair, tag):
-            words = keep.tile([P, PAIR], U32, name="words%d" % pair, tag=tag, align_bytes=64)
+            words = sbuf([P, PAIR], U32, "words%d" % pair, tag)
             nc.vector.tensor_copy(words[:], x_all[:].bitcast(U32).indirect(list_piece(pair * PAIR, PAIR)))
             slot_words[pair] = words
 
-        out_blocks = out.rearrange("(g p) (m c) -> g p m c", p=P, m=RANKS)
-        hidden = {}
-        codes = {}
+        def layer1(e, m):
+            part = e // 2 * RANKS + m
+            if part not in hidden:
+                hidden[part] = sbuf([P, 2, U, PACK], BF16, "h%d" % part)
+            w1_plane = s1_turned[:] if e == 0 else s1_plane[:, e, :]
+            in_pair = (e % 2) * C + m * U
+            slot = e * C + m * U
+            a = bank(A_BANK[len(done)], [P, PACK, U], "a")
+            done.append((e, m))
+            for t in range(PACK):
+                nc.tensor.matmul_mx(
+                    out=a[:, t, :],
+                    lhsT=w1_turned[e // 2][:, t, e % 2, :].bitcast(FP4X4),
+                    lhsT_scale=w1_plane[:, t * P // 4 : (t + 1) * P // 4].bitcast(U8),
+                    rhs=slot_words[e // 2][:, in_pair : in_pair + U].bitcast(FP8X4),
+                    rhs_scale=x_plane[:, slot // 4 : (slot + U) // 4].bitcast(U8),
+                    start=True,
+                    stop=True,
+                )
+            nc.scalar.activation(hidden[part][:, e % 2, :, :], a[:].rearrange("p t u -> p u t"), SILU)
 
-        def layer1(e):
-            h = keep.tile([P, C, PACK], BF16, name="h%d" % e, tag="h%d" % e, align_bytes=64)
-            for m in range(RANKS):
-                in_pair = (e % 2) * C + m * U
-                slot = e * C + m * U
-                a = bank((FIRST_BANKS + LATER_BANKS)[RANKS * e + m], [P, PACK, U], "a")
-                for t in range(PACK):
-                    nc.tensor.matmul_mx(
-                        out=a[:, t, :],
-                        lhsT=w1_turned[e // 2][:, t, e % 2, :].bitcast(FP4X4),
-                        lhsT_scale=s1_plane[:, e, t * P // 4 : (t + 1) * P // 4].bitcast(U8),
-                        rhs=slot_words[e // 2][:, in_pair : in_pair + U].bitcast(FP8X4),
-                        rhs_scale=x_plane[:, slot // 4 : (slot + U) // 4].bitcast(U8),
-                        start=True,
-                        stop=True,
-                    )
-                nc.scalar.activation(h[:, m * U : (m + 1) * U, :], a[:].rearrange("p t u -> p u t"), SILU)
-            hidden[e] = h
+        def layer1_rank(pair, m):
+            layer1(2 * pair, m)
+            layer1(2 * pair + 1, m)
 
-        def quantise(values, width, name):
-            h_words = keep.tile([P, width], U32, name=name, tag=name, align_bytes=64)
-            h_plane = keep.tile([P, width], U8, name=name + "_plane", align_bytes=64)
+        def quantise(values, width, name, tag=None):
+            h_words = sbuf([P, width], U32, name, tag)
+            h_plane = sbuf([P, width], U8, name + "_plane")
             nc.vector.quantize_mx(
                 out=h_words[:].bitcast(FP8X4), scales=h_plane[:], in_=values.rearrange("p c t -> p (c t)")
             )
@@ -181,64 +176,106 @@ def tile_moe_pke_mlp_silu_kernel(tc, x_words, x_scales, w1_words, w1_scales, w2_
             else:
                 nc.vector.tensor_copy(staged, y)
 
-        def quantise_expert(e):
-            codes[e] = quantise(hidden[e][:], C, "h_words%d" % e)
+        def quantise_part(part, tag=None):
+            codes[part] = quantise(hidden[part][:].rearrange("p j u t -> p (j u) t"), C, "h_words%d" % part, tag)
 
-        def layer2(e):
-            cols = slice(e * U, (e + 1) * U)
-            h_words, h_plane = codes[e]
-            y = bank(Y_BANK[e], [P, G, C], "y")
-            for g in range(G):
-                product2(e, g, h_words, h_plane, y[:, g, :])
-            staged = keep.tile([P, G, RANKS, U], F32, name="staged%d" % e)
-            copy_out(e in SCALAR_ONLY, staged[:], y[:].rearrange("p g (m u) -> p g m u", m=RANKS))
-            for g in range(G):
-                nc.sync.dma_start(out_blocks[g, :, :, cols], staged[:, g, :, :])
+        def layer2(part):
+            h_words, h_plane = codes[part]
+            sums[part] = bank(Y_BANK[part], [P, G, 2, U], "y")
+            for j in range(2):
+                cols = slice(j * U, (j + 1) * U)
+                for g in range(G):
+                    product2(part // 2 * 2 + j, g, h_words[:, cols], h_plane[:, cols], sums[part][:, g, j, :])
 
-        def layer2_by_rank(e):
-            cols = slice(e * U, (e + 1) * U)
-            h_words, h_plane = quantise(hidden[e][:, 0:U, :], U, "h_words_rank0")
+        def store(part):
+            pair, m = divmod(part, RANKS)
+            staged = sbuf([P, G, C], F32, "staged%d" % part)
+            sums[part, "staged"] = staged
+            copy_out(part in SCALAR_ONLY, staged[:], sums[part][:].rearrange("p g j u -> p g (j u)"))
+            nc.sync.dma_start(out_blocks[:, :, m, pair * C : (pair + 1) * C].rearrange("g p c -> p g c"), staged[:])
+
+        def last_but_one():
+            e, m = E - 2, RANKS - 1
+            h_words, h_plane = quantise(hidden[E - 1][:, 0, :, :], U, "h_words_a")
             y = bank(LAST_BANKS[0], [P, G, U], "y")
-            staged = keep.tile([P, G, U], F32, name="staged_rank0")
+            staged = sbuf([P, G, U], F32, "staged_a")
             for g in range(G):
                 product2(e, g, h_words, h_plane, y[:, g, :])
-            nc.vector.tensor_copy(staged[:], y[:])
-            nc.sync.dma_start(out_blocks[:, :, 0, cols].rearrange("g p u -> p g u"), staged[:])
-            h_words, h_plane = quantise(hidden[e][:, U:C, :], U, "h_words_rank1")
+            copy_out(A_ON_SCALAR, staged[:], y[:])
+            nc.sync.dma_start(out_blocks[:, :, m, e * U : (e + 1) * U].rearrange("g p u -> p g u"), staged[:])
+
+        def last():
+            e, m = E - 1, RANKS - 1
+            h_words, h_plane = quantise(hidden[E - 1][:, 1, :, :], U, "h_words_b")
             for g, queue in enumerate((nc.sync, nc.scalar)):
                 y = bank(LAST_BANKS[1 + g], [P, U], "y")
-                staged = keep.tile([P, U], F32, name="staged_rank1_%d" % g)
+                staged = sbuf([P, U], F32, "staged_b%d" % g)
                 product2(e, g, h_words, h_plane, y[:])
                 copy_out(g == 1, staged[:], y[:])
-                queue.dma_start(out_blocks[g, :, 1, cols], staged[:])
+                queue.dma_start(out_blocks[g, :, m, e * U : (e + 1) * U], staged[:])
 
+        nc.vector.memset(x_rows[:], 0)
+        nc.vector.memset(x_plane[:], 0)
+        nc.vector.memset(s1_plane[:], 0)
+        nc.vector.memset(warm_in[:], 0.0)
+        nc.sync.dma_start(offsets[:], offs)
+        for q, queue in enumerate((nc.sync, nc.sync, nc.scalar, nc.scalar)):
+            load_s1(q, queue)
+        load_w1(0)
+        load_token_scales()
+        load_tokens(0, 7 * T // 8)
+        nc.scalar.activation(warm_out[:], warm_in[:], SILU)
+        permute_scales()
+        permute(0)
+        rows_first = gather_rows(0, PAIR, "rows_first")
+        rows_second = gather_rows(PAIR, E * C - PAIR, "rows_second")
+        spread_rows(rows_first, 0, PAIR)
+        load_tokens(7 * T // 8, T)
+        load_w1(1)
+        spread_s1()
+        spread_rows(rows_second, PAIR, E * C - PAIR)
+        load_s2()
+        load_w1(2)
+        load_w2(0)
+        load_w1(3)
+        load_w2(1)
         gather(0, "words0")
         gather(1, "words1")
         permute(1)
-        layer1(0)
-        layer1(1)
-        quantise_expert(0)
-        gather(2, "words0")
+        gather(2, "w1_raw1")
+        layer1(0, 0)
+        layer1(0, 1)
+        layer1(1, 0)
+        layer1(1, 1)
+        quantise_part(0)
+        layer1_rank(1, 0)
+        quantise_part(1, "codes")
+        layer1_rank(1, 1)
         permute(2)
-        layer1(2)
-        quantise_expert(1)
-        layer1(3)
-        gather(3, "words1")
-        quantise_expert(2)
-        quantise_expert(3)
         layer2(0)
-        permute(3)
         layer2(1)
-        layer1(4)
+        store(0)
+        store(1)
+        quantise_part(2, "codes")
         layer2(2)
-        quantise_expert(4)
+        layer1_rank(2, 0)
+        gather(3, "h2")
+        quantise_part(3, "codes")
         layer2(3)
-        layer1(5)
-        quantise_expert(5)
+        store(2)
+        layer1_rank(2, 1)
+        permute(3)
+        quantise_part(4)
+        store(3)
+        layer1_rank(3, 0)
         layer2(4)
-        layer1(6)
-        quantise_expert(6)
+        quantise_part(5)
+        store(4)
+        layer1_rank(3, 1)
         layer2(5)
-        layer1(7)
+        quantise_part(6)
+        store(5)
         layer2(6)
-        layer2_by_rank(7)
+        last_but_one()
+        store(6)
+        last()

@@ -22,12 +22,14 @@ U = C // RANKS
 G = N // P
 PAIR = 2 * C
 HALF = E * C // 2
+ROW0 = P - K // 32
+SPAN = 2 * C * PACK
 LINE = 8
-SCALAR_ONLY = (1, 5, 6)
-A_ON_SCALAR = False
-A_BANK = (0, 1, 2, 3, 4, 5, 6, 7, 4, 5, 6, 7, 0, 1, 4, 5)
-Y_BANK = (0, 1, 2, 3, 6, 7, 0)
-LAST_BANKS = (1, 2, 3)
+SCALAR_ONLY = (5,)
+A_ON_SCALAR = True
+A_BANK = (0, 1, 2, 3, 4, 5, 6, 7, 4, 5, 6, 7, 0, 4, 5, 6)
+Y_BANK = (0, 1, 2, 3, 7, 0, 4)
+LAST_BANKS = (5, 1, 2)
 FLOPS = 2 * E * C * (K * H + H * N)
 
 
@@ -35,23 +37,26 @@ def tile_moe_pke_mlp_silu_kernel(tc, x_words, x_scales, w1_words, w1_scales, w2_
     nc = tc.nc
     with ExitStack() as ctx:
         keep = ctx.enter_context(tc.tile_pool(name="keep", bufs=1))
+        turns = ctx.enter_context(tc.tile_pool(name="turns", bufs=1))
         psum = ctx.enter_context(tc.psum_pool(name="psum", bufs=1))
 
         def bank(number, shape, name):
             return psum.tile(shape, F32, name=name, tag="bank%d" % number)
 
-        def sbuf(shape, dtype, name, tag=None):
+        def sbuf(shape, dtype, name, tag=None, offset=None):
+            if offset is not None:
+                return turns.tile(shape, dtype, name=name, offset=offset, align_bytes=64)
             return keep.tile(shape, dtype, name=name, tag=tag or name, align_bytes=64)
 
         offsets = keep.tile([P, E * C // 16], U16, name="offsets")
         x_all = sbuf([P, T], I32, "x_all")
-        x_rows = sbuf([P, T // 4], I32, "x_rows")
+        x_rows = turns.tile([P, T // 4], I32, name="x_rows", offset=0, align_bytes=64)
         s1_raw = sbuf([P, H // 4], I32, "s1_raw")
         s1_turned = sbuf([P, H // 4], I32, "s1_turned")
         s1_plane = sbuf([P, E, H // 4], I32, "s1_plane")
-        w1_raw = [sbuf([P, 2, H // 2], I32, "w1_raw%d" % pair) for pair in range(E // 2)]
+        w1_raw = {}
         w2 = [sbuf([P, E // 2, N // 2], I32, "w2_%d" % half) for half in range(2)]
-        x_plane = sbuf([P, E * C // 4], I32, "x_plane")
+        x_planes = []
         warm_in = keep.tile([P, 1], F32, name="warm_in")
         warm_out = keep.tile([P, 1], F32, name="warm_out")
 
@@ -60,7 +65,7 @@ def tile_moe_pke_mlp_silu_kernel(tc, x_words, x_scales, w1_words, w1_scales, w2_
         w2_hbm = w2_words.rearrange("e s p b -> p (e s) b").bitcast(I32)
         s2_hbm = w2_scales.rearrange("e s q i -> q (e s) i").bitcast(I32)
         out_blocks = out.rearrange("(g p) (m c) -> g p m c", p=P, m=RANKS)
-        s2_plane = w1_raw[0][:].rearrange("p a (b c) -> p (a b) c", c=N // 4)
+        s2_plane = turns.tile([P, E, N // 4], I32, name="s2_plane", offset=0, align_bytes=64)
         w1_turned = {}
         slot_words = {}
         hidden = {}
@@ -71,8 +76,9 @@ def tile_moe_pke_mlp_silu_kernel(tc, x_words, x_scales, w1_words, w1_scales, w2_
         def load_tokens(first, last):
             nc.sync.dma_start(x_all[:, first:last], x_hbm[:, first:last])
 
-        def load_w1(pair):
-            nc.sync.dma_start(w1_raw[pair][:], w1_hbm[:, 2 * pair : 2 * pair + 2, :])
+        def load_w1(first, count):
+            w1_raw[first] = sbuf([P, count, H // 2], I32, "w1_raw%d" % first, offset=T + SPAN // 2 if first == 2 else None)
+            nc.sync.dma_start(w1_raw[first][:], w1_hbm[:, first : first + count, :])
 
         def load_w2(half):
             nc.sync.dma_start(w2[half][:], w2_hbm[:, half * E // 2 : (half + 1) * E // 2, :])
@@ -87,7 +93,7 @@ def tile_moe_pke_mlp_silu_kernel(tc, x_words, x_scales, w1_words, w1_scales, w2_
                 nc.sync.dma_start(s2_plane[r:P:QUAD, :, :], s2_hbm[r : K // 32 : ROWS, :, :])
 
         def load_token_scales():
-            nc.sync.dma_start(x_rows[0:P:8, :], x_scales[0].bitcast(I32))
+            nc.sync.dma_start(x_rows[ROW0:P, :], x_scales[0].bitcast(I32))
 
         def permute_scales():
             nc.vector.tensor_copy(
@@ -95,12 +101,15 @@ def tile_moe_pke_mlp_silu_kernel(tc, x_words, x_scales, w1_words, w1_scales, w2_
                 s1_raw[:].bitcast(U8).rearrange("p (m t) -> p t m", t=PACK),
             )
 
-        def permute(pair):
-            w1_turned[pair] = sbuf([P, PACK, 2, P // 2], I32, "w1_turned%d" % pair)
-            nc.vector.tensor_copy(
-                w1_turned[pair][:].bitcast(U16).rearrange("p t e (a b) -> p (e a) t b", b=LINE),
-                w1_raw[pair][:].bitcast(U16).rearrange("p e (a b t) -> p (e a) t b", b=LINE, t=PACK),
+        def permute(first, copy):
+            count = w1_raw[first].shape[1]
+            turned = sbuf([P, PACK, count, P // 2], I32, "w1_turned%d" % first)
+            copy(
+                turned[:].bitcast(U16).rearrange("p t e (a b) -> p (e a) t b", b=LINE),
+                w1_raw[first][:].bitcast(U16).rearrange("p e (a b t) -> p (e a) t b", b=LINE, t=PACK),
             )
+            for j in range(count):
+                w1_turned[first + j] = turned[:, :, j, :]
 
         def spread_s1():
             for r in range(ROWS):
@@ -114,11 +123,12 @@ def tile_moe_pke_mlp_silu_kernel(tc, x_words, x_scales, w1_words, w1_scales, w2_
             nc.vector.tensor_copy(rows[:], x_rows[:].bitcast(U8).indirect(list_piece(first, count)))
             return rows
 
-        def spread_rows(rows, first, count):
+        def spread_rows(rows, plane):
+            x_planes.append(plane)
             for r in range(ROWS):
                 nc.sync.dma_start(
-                    x_plane[r:P:QUAD, first // 4 : (first + count) // 4],
-                    rows[8 * r : P : QUAD, :].bitcast(I32),
+                    plane[r:P:QUAD, :],
+                    rows[ROW0 + r : P : ROWS, :].bitcast(I32),
                 )
 
         def gather(pair, tag):
@@ -129,19 +139,21 @@ def tile_moe_pke_mlp_silu_kernel(tc, x_words, x_scales, w1_words, w1_scales, w2_
         def layer1(e, m):
             part = e // 2 * RANKS + m
             if part not in hidden:
-                hidden[part] = sbuf([P, 2, U, PACK], BF16, "h%d" % part)
+                hidden[part] = sbuf([P, 2, U, PACK], BF16, "h%d" % part, offset=T + part * SPAN if part < RANKS else None)
             w1_plane = s1_turned[:] if e == 0 else s1_plane[:, e, :]
             in_pair = (e % 2) * C + m * U
             slot = e * C + m * U
+            late = slot >= PAIR
+            x_scale = x_planes[late][:, (slot - late * PAIR) // 4 : (slot - late * PAIR + U) // 4]
             a = bank(A_BANK[len(done)], [P, PACK, U], "a")
             done.append((e, m))
             for t in range(PACK):
                 nc.tensor.matmul_mx(
                     out=a[:, t, :],
-                    lhsT=w1_turned[e // 2][:, t, e % 2, :].bitcast(FP4X4),
+                    lhsT=w1_turned[e][:, t, :].bitcast(FP4X4),
                     lhsT_scale=w1_plane[:, t * P // 4 : (t + 1) * P // 4].bitcast(U8),
                     rhs=slot_words[e // 2][:, in_pair : in_pair + U].bitcast(FP8X4),
-                    rhs_scale=x_plane[:, slot // 4 : (slot + U) // 4].bitcast(U8),
+                    rhs_scale=x_scale.bitcast(U8),
                     start=True,
                     stop=True,
                 )
@@ -187,9 +199,9 @@ def tile_moe_pke_mlp_silu_kernel(tc, x_words, x_scales, w1_words, w1_scales, w2_
                 for g in range(G):
                     product2(part // 2 * 2 + j, g, h_words[:, cols], h_plane[:, cols], sums[part][:, g, j, :])
 
-        def store(part):
+        def store(part, tag=None):
             pair, m = divmod(part, RANKS)
-            staged = sbuf([P, G, C], F32, "staged%d" % part)
+            staged = sbuf([P, G, C], F32, "staged%d" % part, tag)
             sums[part, "staged"] = staged
             copy_out(part in SCALAR_ONLY, staged[:], sums[part][:].rearrange("p g j u -> p g (j u)"))
             nc.sync.dma_start(out_blocks[:, :, m, pair * C : (pair + 1) * C].rearrange("g p c -> p g c"), staged[:])
@@ -214,35 +226,36 @@ def tile_moe_pke_mlp_silu_kernel(tc, x_words, x_scales, w1_words, w1_scales, w2_
                 copy_out(g == 1, staged[:], y[:])
                 queue.dma_start(out_blocks[g, :, m, e * U : (e + 1) * U], staged[:])
 
-        nc.vector.memset(x_rows[:], 0)
-        nc.vector.memset(x_plane[:], 0)
-        nc.vector.memset(s1_plane[:], 0)
         nc.vector.memset(warm_in[:], 0.0)
-        nc.sync.dma_start(offsets[:], offs)
+        nc.vector.memset(x_rows[0:ROW0, :], 0)
+        nc.vector.memset(s1_plane[:], 0)
         for q, queue in enumerate((nc.sync, nc.sync, nc.scalar, nc.scalar)):
             load_s1(q, queue)
-        load_w1(0)
         load_token_scales()
+        nc.sync.dma_start(offsets[:], offs)
+        load_w1(0, 1)
         load_tokens(0, 7 * T // 8)
         nc.scalar.activation(warm_out[:], warm_in[:], SILU)
         permute_scales()
-        permute(0)
         rows_first = gather_rows(0, PAIR, "rows_first")
+        permute(0, nc.scalar.copy)
         rows_second = gather_rows(PAIR, E * C - PAIR, "rows_second")
-        spread_rows(rows_first, 0, PAIR)
+        spread_rows(rows_first, sbuf([P, PAIR // 4], I32, "x_plane_first", "s1_raw"))
         load_tokens(7 * T // 8, T)
-        load_w1(1)
+        load_w1(1, 1)
+        load_w1(2, 2)
         spread_s1()
-        spread_rows(rows_second, PAIR, E * C - PAIR)
+        spread_rows(rows_second, turns.tile([P, (E * C - PAIR) // 4], I32, name="x_plane_second", offset=E * N, align_bytes=64))
         load_s2()
-        load_w1(2)
+        load_w1(4, 2)
         load_w2(0)
-        load_w1(3)
+        load_w1(6, 2)
         load_w2(1)
-        gather(0, "words0")
-        gather(1, "words1")
-        permute(1)
-        gather(2, "w1_raw1")
+        gather(0, "w1_raw0")
+        permute(1, nc.scalar.copy)
+        permute(2, nc.scalar.copy)
+        for pair in range(1, E // 2):
+            gather(pair, "words%d" % pair)
         layer1(0, 0)
         layer1(0, 1)
         layer1(1, 0)
@@ -251,31 +264,30 @@ def tile_moe_pke_mlp_silu_kernel(tc, x_words, x_scales, w1_words, w1_scales, w2_
         layer1_rank(1, 0)
         quantise_part(1, "codes")
         layer1_rank(1, 1)
-        permute(2)
+        permute(4, nc.vector.tensor_copy)
         layer2(0)
         layer2(1)
         store(0)
-        store(1)
         quantise_part(2, "codes")
         layer2(2)
         layer1_rank(2, 0)
-        gather(3, "h2")
         quantise_part(3, "codes")
         layer2(3)
-        store(2)
         layer1_rank(2, 1)
-        permute(3)
+        permute(6, nc.vector.tensor_copy)
+        store(1)
         quantise_part(4)
-        store(3)
+        store(2)
         layer1_rank(3, 0)
         layer2(4)
         quantise_part(5)
-        store(4)
+        store(3)
         layer1_rank(3, 1)
         layer2(5)
         quantise_part(6)
-        store(5)
+        store(4)
         layer2(6)
+        store(5)
         last_but_one()
         store(6)
         last()

@@ -25,11 +25,9 @@ HALF = E * C // 2
 ROW0 = P - K // 32
 SPAN = 2 * C * PACK
 LINE = 8
-SCALAR_ONLY = (5,)
-A_ON_SCALAR = True
 A_BANK = (0, 1, 2, 3, 4, 5, 6, 7, 4, 5, 6, 7, 0, 4, 5, 6)
-Y_BANK = (0, 1, 2, 3, 7, 0, 4)
-LAST_BANKS = (5, 1, 2)
+Y_BANK = (0, 1, 2, 3, 7, 0)
+LAST_BANKS = (5, 3)
 FLOPS = 2 * E * C * (K * H + H * N)
 
 
@@ -55,7 +53,7 @@ def tile_moe_pke_mlp_silu_kernel(tc, x_words, x_scales, w1_words, w1_scales, w2_
         s1_turned = sbuf([P, H // 4], I32, "s1_turned")
         s1_plane = sbuf([P, E, H // 4], I32, "s1_plane")
         w1_raw = {}
-        w2 = [sbuf([P, E // 2, N // 2], I32, "w2_%d" % half) for half in range(2)]
+        w2 = {}
         x_planes = []
         warm_in = keep.tile([P, 1], F32, name="warm_in")
         warm_out = keep.tile([P, 1], F32, name="warm_out")
@@ -80,8 +78,11 @@ def tile_moe_pke_mlp_silu_kernel(tc, x_words, x_scales, w1_words, w1_scales, w2_
             w1_raw[first] = sbuf([P, count, H // 2], I32, "w1_raw%d" % first, offset=T + SPAN // 2 if first == 2 else None)
             nc.sync.dma_start(w1_raw[first][:], w1_hbm[:, first : first + count, :])
 
-        def load_w2(half):
-            nc.sync.dma_start(w2[half][:], w2_hbm[:, half * E // 2 : (half + 1) * E // 2, :])
+        def load_w2(first, count):
+            words = sbuf([P, count, N // 2], I32, "w2_%d" % first)
+            nc.sync.dma_start(words[:], w2_hbm[:, first : first + count, :])
+            for j in range(count):
+                w2[first + j] = words[:, j, :]
 
         def load_s1(q, queue):
             queue.dma_start(
@@ -174,7 +175,7 @@ def tile_moe_pke_mlp_silu_kernel(tc, x_words, x_scales, w1_words, w1_scales, w2_
         def product2(e, g, h_words, h_plane, y):
             nc.tensor.matmul_mx(
                 out=y,
-                lhsT=w2[e // (E // 2)][:, e % (E // 2), g * P // 2 : (g + 1) * P // 2].bitcast(FP4X4),
+                lhsT=w2[e][:, g * P // 2 : (g + 1) * P // 2].bitcast(FP4X4),
                 lhsT_scale=s2_plane[:, e, g * P // 4 : (g + 1) * P // 4].bitcast(U8),
                 rhs=h_words.bitcast(FP8X4),
                 rhs_scale=h_plane,
@@ -199,28 +200,32 @@ def tile_moe_pke_mlp_silu_kernel(tc, x_words, x_scales, w1_words, w1_scales, w2_
                 for g in range(G):
                     product2(part // 2 * 2 + j, g, h_words[:, cols], h_plane[:, cols], sums[part][:, g, j, :])
 
-        def store(part, tag=None):
+        def store(part, on_scalar=False, tag=None):
             pair, m = divmod(part, RANKS)
             staged = sbuf([P, G, C], F32, "staged%d" % part, tag)
             sums[part, "staged"] = staged
-            copy_out(part in SCALAR_ONLY, staged[:], sums[part][:].rearrange("p g j u -> p g (j u)"))
+            copy_out(on_scalar, staged[:], sums[part][:].rearrange("p g j u -> p g (j u)"))
             nc.sync.dma_start(out_blocks[:, :, m, pair * C : (pair + 1) * C].rearrange("g p c -> p g c"), staged[:])
 
-        def last_but_one():
-            e, m = E - 2, RANKS - 1
-            h_words, h_plane = quantise(hidden[E - 1][:, 0, :, :], U, "h_words_a")
-            y = bank(LAST_BANKS[0], [P, G, U], "y")
-            staged = sbuf([P, G, U], F32, "staged_a")
+        def quantise_half(e, m):
+            codes[e, m] = quantise(hidden[e // 2 * RANKS + m][:, e % 2, :, :], U, "h_words%d_%d" % (e, m))
+
+        def layer2_half(e, m, number):
+            h_words, h_plane = codes[e, m]
+            sums[e, m] = bank(number, [P, G, U], "y")
             for g in range(G):
-                product2(e, g, h_words, h_plane, y[:, g, :])
-            copy_out(A_ON_SCALAR, staged[:], y[:])
+                product2(e, g, h_words, h_plane, sums[e, m][:, g, :])
+
+        def store_half(e, m, on_scalar):
+            staged = sbuf([P, G, U], F32, "staged%d_%d" % (e, m))
+            copy_out(on_scalar, staged[:], sums[e, m][:])
             nc.sync.dma_start(out_blocks[:, :, m, e * U : (e + 1) * U].rearrange("g p u -> p g u"), staged[:])
 
         def last():
             e, m = E - 1, RANKS - 1
-            h_words, h_plane = quantise(hidden[E - 1][:, 1, :, :], U, "h_words_b")
+            h_words, h_plane = codes[e, m]
             for g, queue in enumerate((nc.sync, nc.scalar)):
-                y = bank(LAST_BANKS[1 + g], [P, U], "y")
+                y = bank(LAST_BANKS[g], [P, U], "y")
                 staged = sbuf([P, U], F32, "staged_b%d" % g)
                 product2(e, g, h_words, h_plane, y[:])
                 copy_out(g == 1, staged[:], y[:])
@@ -248,9 +253,10 @@ def tile_moe_pke_mlp_silu_kernel(tc, x_words, x_scales, w1_words, w1_scales, w2_
         spread_rows(rows_second, turns.tile([P, (E * C - PAIR) // 4], I32, name="x_plane_second", offset=E * N, align_bytes=64))
         load_s2()
         load_w1(4, 2)
-        load_w2(0)
+        load_w2(0, 2)
         load_w1(6, 2)
-        load_w2(1)
+        load_w2(2, 2)
+        load_w2(4, 4)
         gather(0, "w1_raw0")
         permute(1, nc.scalar.copy)
         permute(2, nc.scalar.copy)
@@ -284,10 +290,16 @@ def tile_moe_pke_mlp_silu_kernel(tc, x_words, x_scales, w1_words, w1_scales, w2_
         store(3)
         layer1_rank(3, 1)
         layer2(5)
-        quantise_part(6)
+        quantise_half(6, 0)
+        quantise_half(7, 0)
+        layer2_half(6, 0, 1)
+        layer2_half(7, 0, 4)
+        quantise_half(6, 1)
+        quantise_half(7, 1)
+        layer2_half(6, 1, 2)
         store(4)
-        layer2(6)
-        store(5)
-        last_but_one()
-        store(6)
+        store(5, True)
+        store_half(6, 0, False)
+        store_half(7, 0, False)
+        store_half(6, 1, True)
         last()

@@ -75,7 +75,7 @@ def tile_moe_pke_mlp_silu_kernel(tc, x_words, x_scales, w1_words, w1_scales, w2_
             nc.sync.dma_start(x_all[:, first:last], x_hbm[:, first:last])
 
         def load_w1(first, count):
-            w1_raw[first] = sbuf([P, count, H // 2], I32, "w1_raw%d" % first, offset=T + SPAN // 2 if first == 2 else None)
+            w1_raw[first] = sbuf([P, count, H // 2], I32, "w1_raw%d" % first)
             nc.sync.dma_start(w1_raw[first][:], w1_hbm[:, first : first + count, :])
 
         def load_w2(first, count):
@@ -124,23 +124,23 @@ def tile_moe_pke_mlp_silu_kernel(tc, x_words, x_scales, w1_words, w1_scales, w2_
             nc.vector.tensor_copy(rows[:], x_rows[:].bitcast(U8).indirect(list_piece(first, count)))
             return rows
 
-        def spread_rows(rows, plane):
-            x_planes.append(plane)
-            for r in range(ROWS):
+        def spread_rows(rows, plane, first=0, last=ROWS):
+            for r in range(first, last):
                 nc.sync.dma_start(
                     plane[r:P:QUAD, :],
                     rows[ROW0 + r : P : ROWS, :].bitcast(I32),
                 )
 
-        def gather(pair, tag):
-            words = sbuf([P, PAIR], U32, "words%d" % pair, tag)
-            nc.vector.tensor_copy(words[:], x_all[:].bitcast(U32).indirect(list_piece(pair * PAIR, PAIR)))
-            slot_words[pair] = words
+        def gather(pair, count, tag=None):
+            words = sbuf([P, count * PAIR], U32, "words%d" % pair, tag)
+            nc.vector.tensor_copy(words[:], x_all[:].bitcast(U32).indirect(list_piece(pair * PAIR, count * PAIR)))
+            for j in range(count):
+                slot_words[pair + j] = words[:, j * PAIR : (j + 1) * PAIR]
 
         def layer1(e, m):
             part = e // 2 * RANKS + m
             if part not in hidden:
-                hidden[part] = sbuf([P, 2, U, PACK], BF16, "h%d" % part, offset=T + part * SPAN if part < RANKS else None)
+                hidden[part] = sbuf([P, 2, U, PACK], BF16, "h%d" % part)
             w1_plane = s1_turned[:] if e == 0 else s1_plane[:, e, :]
             in_pair = (e % 2) * C + m * U
             slot = e * C + m * U
@@ -239,29 +239,31 @@ def tile_moe_pke_mlp_silu_kernel(tc, x_words, x_scales, w1_words, w1_scales, w2_
         load_token_scales()
         nc.sync.dma_start(offsets[:], offs)
         load_w1(0, 1)
-        load_tokens(0, 7 * T // 8)
+        load_tokens(0, T)
         nc.scalar.activation(warm_out[:], warm_in[:], SILU)
         permute_scales()
         rows_first = gather_rows(0, PAIR, "rows_first")
         permute(0, nc.scalar.copy)
         rows_second = gather_rows(PAIR, E * C - PAIR, "rows_second")
-        spread_rows(rows_first, sbuf([P, PAIR // 4], I32, "x_plane_first", "s1_raw"))
-        load_tokens(7 * T // 8, T)
         load_w1(1, 1)
+        x_planes.append(sbuf([P, PAIR // 4], I32, "x_plane_first", "s1_raw"))
+        spread_rows(rows_first, x_planes[0], 0, ROWS - 1)
         load_w1(2, 2)
+        spread_rows(rows_first, x_planes[0], ROWS - 1)
         spread_s1()
-        spread_rows(rows_second, turns.tile([P, (E * C - PAIR) // 4], I32, name="x_plane_second", offset=E * N, align_bytes=64))
+        x_planes.append(sbuf([P, (E * C - PAIR) // 4], I32, "x_plane_second", offset=E * N))
+        spread_rows(rows_second, x_planes[1])
         load_s2()
         load_w1(4, 2)
         load_w2(0, 2)
         load_w1(6, 2)
         load_w2(2, 2)
         load_w2(4, 4)
-        gather(0, "w1_raw0")
+        gather(0, 1, "w1_raw0")
         permute(1, nc.scalar.copy)
         permute(2, nc.scalar.copy)
-        for pair in range(1, E // 2):
-            gather(pair, "words%d" % pair)
+        gather(1, 1)
+        gather(2, 2)
         layer1(0, 0)
         layer1(0, 1)
         layer1(1, 0)

@@ -239,15 +239,16 @@ def tile_moe_pke_mlp_silu_kernel(tc, x_words, x_scales, w1_words, w1_scales, w2_
         load_token_scales()
         nc.sync.dma_start(offsets[:], offs)
         load_w1(0, 1)
-        load_tokens(0, T)
+        load_tokens(0, 7 * T // 8)
         nc.scalar.activation(warm_out[:], warm_in[:], SILU)
         permute_scales()
         rows_first = gather_rows(0, PAIR, "rows_first")
         permute(0, nc.scalar.copy)
         rows_second = gather_rows(PAIR, E * C - PAIR, "rows_second")
-        load_w1(1, 1)
         x_planes.append(sbuf([P, PAIR // 4], I32, "x_plane_first", "s1_raw"))
         spread_rows(rows_first, x_planes[0], 0, ROWS - 1)
+        load_tokens(7 * T // 8, T)
+        load_w1(1, 1)
         load_w1(2, 2)
         spread_rows(rows_first, x_planes[0], ROWS - 1)
         spread_s1()

@@ -21,17 +21,16 @@ RANKS = 2
 U = C // RANKS
 G = N // P
 PAIR = 2 * C
-HALF = E * C // 2
 ROW0 = P - K // 32
-SPAN = 2 * C * PACK
+X_FIRST = 7 * T // 8
 LINE = 8
-A_BANK = (0, 1, 2, 3, 4, 5, 6, 7, 4, 5, 6, 7, 0, 4, 5, 6)
-Y_BANK = (0, 1, 2, 3, 7, 0)
-LAST_BANKS = (5, 3)
+BANKS = 8
 FLOPS = 2 * E * C * (K * H + H * N)
 
 
-def tile_moe_pke_mlp_silu_kernel(tc, x_words, x_scales, w1_words, w1_scales, w2_words, w2_scales, offs, out):
+def tile_moe_pke_mlp_silu_kernel(
+    tc, x_words, x_scales, w1_words, w1_scales, w2_words, w2_scales, offs, out
+):
     nc = tc.nc
     with ExitStack() as ctx:
         keep = ctx.enter_context(tc.tile_pool(name="keep", bufs=1))
@@ -48,31 +47,22 @@ def tile_moe_pke_mlp_silu_kernel(tc, x_words, x_scales, w1_words, w1_scales, w2_
 
         offsets = keep.tile([P, E * C // 16], U16, name="offsets")
         x_all = sbuf([P, T], I32, "x_all")
-        x_rows = turns.tile([P, T // 4], I32, name="x_rows", offset=0, align_bytes=64)
+        x_rows = sbuf([P, T // 4], I32, "x_rows", offset=0)
         s1_raw = sbuf([P, H // 4], I32, "s1_raw")
         s1_turned = sbuf([P, H // 4], I32, "s1_turned")
         s1_plane = sbuf([P, E, H // 4], I32, "s1_plane")
-        w1_raw = {}
-        w2 = {}
-        x_planes = []
         warm_in = keep.tile([P, 1], F32, name="warm_in")
         warm_out = keep.tile([P, 1], F32, name="warm_out")
+        s2_plane = sbuf([P, E, N // 4], I32, "s2_plane", offset=0)
 
         x_hbm = x_words[0].rearrange("p t r -> p (t r)").bitcast(I32)
         w1_hbm = w1_words.rearrange("e s p b -> p (e s) b").bitcast(I32)
         w2_hbm = w2_words.rearrange("e s p b -> p (e s) b").bitcast(I32)
         s2_hbm = w2_scales.rearrange("e s q i -> q (e s) i").bitcast(I32)
         out_blocks = out.rearrange("(g p) (m c) -> g p m c", p=P, m=RANKS)
-        s2_plane = turns.tile([P, E, N // 4], I32, name="s2_plane", offset=0, align_bytes=64)
-        w1_turned = {}
-        slot_words = {}
-        hidden = {}
-        codes = {}
-        sums = {}
-        done = []
-
-        def load_tokens(first, last):
-            nc.sync.dma_start(x_all[:, first:last], x_hbm[:, first:last])
+        w1_raw, w1_turned, w2, slot_words, hidden, codes, sums = {}, {}, {}, {}, {}, {}, {}
+        a_banks = [n if n < BANKS else BANKS // 2 + n % (BANKS // 2) for n in range(E * RANKS)]
+        y_banks = [n % (BANKS // 2) for n in range(E * RANKS)]
 
         def load_w1(first, count):
             w1_raw[first] = sbuf([P, count, H // 2], I32, "w1_raw%d" % first)
@@ -84,24 +74,6 @@ def tile_moe_pke_mlp_silu_kernel(tc, x_words, x_scales, w1_words, w1_scales, w2_
             for j in range(count):
                 w2[first + j] = words[:, j, :]
 
-        def load_s1(q, queue):
-            queue.dma_start(
-                s1_raw[QUAD * q : QUAD * (q + 1), :], w1_scales[:, 0, ROWS * q : ROWS * (q + 1), :].bitcast(I32)
-            )
-
-        def load_s2():
-            for r in range(ROWS):
-                nc.sync.dma_start(s2_plane[r:P:QUAD, :, :], s2_hbm[r : K // 32 : ROWS, :, :])
-
-        def load_token_scales():
-            nc.sync.dma_start(x_rows[ROW0:P, :], x_scales[0].bitcast(I32))
-
-        def permute_scales():
-            nc.vector.tensor_copy(
-                s1_turned[:].bitcast(U8).rearrange("p (t m) -> p t m", t=PACK),
-                s1_raw[:].bitcast(U8).rearrange("p (m t) -> p t m", t=PACK),
-            )
-
         def permute(first, copy):
             count = w1_raw[first].shape[1]
             turned = sbuf([P, PACK, count, P // 2], I32, "w1_turned%d" % first)
@@ -111,10 +83,6 @@ def tile_moe_pke_mlp_silu_kernel(tc, x_words, x_scales, w1_words, w1_scales, w2_
             )
             for j in range(count):
                 w1_turned[first + j] = turned[:, :, j, :]
-
-        def spread_s1():
-            for r in range(ROWS):
-                nc.sync.dma_start(s1_plane[r:P:QUAD, :, :], s1_turned[r:P:ROWS, :])
 
         def list_piece(first, count):
             return offsets[:, first // 16 : (first + count) // 16]
@@ -126,10 +94,7 @@ def tile_moe_pke_mlp_silu_kernel(tc, x_words, x_scales, w1_words, w1_scales, w2_
 
         def spread_rows(rows, plane, first=0, last=ROWS):
             for r in range(first, last):
-                nc.sync.dma_start(
-                    plane[r:P:QUAD, :],
-                    rows[ROW0 + r : P : ROWS, :].bitcast(I32),
-                )
+                nc.sync.dma_start(plane[r:P:QUAD, :], rows[ROW0 + r : P : ROWS, :].bitcast(I32))
 
         def gather(pair, count, tag=None):
             words = sbuf([P, count * PAIR], U32, "words%d" % pair, tag)
@@ -144,10 +109,11 @@ def tile_moe_pke_mlp_silu_kernel(tc, x_words, x_scales, w1_words, w1_scales, w2_
             w1_plane = s1_turned[:] if e == 0 else s1_plane[:, e, :]
             in_pair = (e % 2) * C + m * U
             slot = e * C + m * U
-            late = slot >= PAIR
-            x_scale = x_planes[late][:, (slot - late * PAIR) // 4 : (slot - late * PAIR + U) // 4]
-            a = bank(A_BANK[len(done)], [P, PACK, U], "a")
-            done.append((e, m))
+            if slot < PAIR:
+                x_scale = x_plane_first[:, slot // 4 : (slot + U) // 4]
+            else:
+                x_scale = x_plane_rest[:, (slot - PAIR) // 4 : (slot - PAIR + U) // 4]
+            a = bank(a_banks.pop(0), [P, PACK, U], "a")
             for t in range(PACK):
                 nc.tensor.matmul_mx(
                     out=a[:, t, :],
@@ -160,7 +126,8 @@ def tile_moe_pke_mlp_silu_kernel(tc, x_words, x_scales, w1_words, w1_scales, w2_
                 )
             nc.scalar.activation(hidden[part][:, e % 2, :, :], a[:].rearrange("p t u -> p u t"), SILU)
 
-        def layer1_rank(pair, m):
+        def layer1_part(part):
+            pair, m = divmod(part, RANKS)
             layer1(2 * pair, m)
             layer1(2 * pair + 1, m)
 
@@ -183,126 +150,126 @@ def tile_moe_pke_mlp_silu_kernel(tc, x_words, x_scales, w1_words, w1_scales, w2_
                 stop=True,
             )
 
-        def copy_out(on_scalar, staged, y):
-            if on_scalar:
-                nc.scalar.copy(staged, y)
-            else:
-                nc.vector.tensor_copy(staged, y)
-
         def quantise_part(part, tag=None):
             codes[part] = quantise(hidden[part][:].rearrange("p j u t -> p (j u) t"), C, "h_words%d" % part, tag)
 
-        def layer2(part):
+        def layer2_part(part):
             h_words, h_plane = codes[part]
-            sums[part] = bank(Y_BANK[part], [P, G, 2, U], "y")
+            sums[part] = bank(y_banks.pop(0), [P, G, 2, U], "y")
             for j in range(2):
                 cols = slice(j * U, (j + 1) * U)
                 for g in range(G):
-                    product2(part // 2 * 2 + j, g, h_words[:, cols], h_plane[:, cols], sums[part][:, g, j, :])
+                    product2(part // RANKS * 2 + j, g, h_words[:, cols], h_plane[:, cols], sums[part][:, g, j, :])
 
-        def store(part, on_scalar=False, tag=None):
+        def store_part(part, copy):
             pair, m = divmod(part, RANKS)
-            staged = sbuf([P, G, C], F32, "staged%d" % part, tag)
-            sums[part, "staged"] = staged
-            copy_out(on_scalar, staged[:], sums[part][:].rearrange("p g j u -> p g (j u)"))
+            staged = sbuf([P, G, C], F32, "staged%d" % part)
+            copy(staged[:], sums[part][:].rearrange("p g j u -> p g (j u)"))
             nc.sync.dma_start(out_blocks[:, :, m, pair * C : (pair + 1) * C].rearrange("g p c -> p g c"), staged[:])
 
         def quantise_half(e, m):
             codes[e, m] = quantise(hidden[e // 2 * RANKS + m][:, e % 2, :, :], U, "h_words%d_%d" % (e, m))
 
-        def layer2_half(e, m, number):
+        def layer2_half(e, m):
             h_words, h_plane = codes[e, m]
-            sums[e, m] = bank(number, [P, G, U], "y")
+            sums[e, m] = bank(y_banks.pop(0), [P, G, U], "y")
             for g in range(G):
                 product2(e, g, h_words, h_plane, sums[e, m][:, g, :])
 
-        def store_half(e, m, on_scalar):
+        def store_half(e, m, copy):
             staged = sbuf([P, G, U], F32, "staged%d_%d" % (e, m))
-            copy_out(on_scalar, staged[:], sums[e, m][:])
+            copy(staged[:], sums[e, m][:])
             nc.sync.dma_start(out_blocks[:, :, m, e * U : (e + 1) * U].rearrange("g p u -> p g u"), staged[:])
 
-        def last():
-            e, m = E - 1, RANKS - 1
-            h_words, h_plane = codes[e, m]
-            for g, queue in enumerate((nc.sync, nc.scalar)):
-                y = bank(LAST_BANKS[g], [P, U], "y")
-                staged = sbuf([P, U], F32, "staged_b%d" % g)
-                product2(e, g, h_words, h_plane, y[:])
-                copy_out(g == 1, staged[:], y[:])
-                queue.dma_start(out_blocks[g, :, m, e * U : (e + 1) * U], staged[:])
+        on_vector, on_scalar = nc.vector.tensor_copy, nc.scalar.copy
 
         nc.vector.memset(warm_in[:], 0.0)
         nc.vector.memset(x_rows[0:ROW0, :], 0)
         nc.vector.memset(s1_plane[:], 0)
         for q, queue in enumerate((nc.sync, nc.sync, nc.scalar, nc.scalar)):
-            load_s1(q, queue)
-        load_token_scales()
+            queue.dma_start(
+                s1_raw[QUAD * q : QUAD * (q + 1), :], w1_scales[:, 0, ROWS * q : ROWS * (q + 1), :].bitcast(I32)
+            )
+        nc.sync.dma_start(x_rows[ROW0:P, :], x_scales[0].bitcast(I32))
         nc.sync.dma_start(offsets[:], offs)
         load_w1(0, 1)
-        load_tokens(0, 7 * T // 8)
+        nc.sync.dma_start(x_all[:, 0:X_FIRST], x_hbm[:, 0:X_FIRST])
         nc.scalar.activation(warm_out[:], warm_in[:], SILU)
-        permute_scales()
+
+        nc.vector.tensor_copy(
+            s1_turned[:].bitcast(U8).rearrange("p (t m) -> p t m", t=PACK),
+            s1_raw[:].bitcast(U8).rearrange("p (m t) -> p t m", t=PACK),
+        )
         rows_first = gather_rows(0, PAIR, "rows_first")
-        permute(0, nc.scalar.copy)
-        rows_second = gather_rows(PAIR, E * C - PAIR, "rows_second")
-        x_planes.append(sbuf([P, PAIR // 4], I32, "x_plane_first", "s1_raw"))
-        spread_rows(rows_first, x_planes[0], 0, ROWS - 1)
-        load_tokens(7 * T // 8, T)
+        permute(0, on_scalar)
+        rows_rest = gather_rows(PAIR, E * C - PAIR, "rows_rest")
+        x_plane_first = sbuf([P, PAIR // 4], I32, "x_plane_first", "s1_raw")
+        spread_rows(rows_first, x_plane_first, 0, ROWS - 1)
+        nc.sync.dma_start(x_all[:, X_FIRST:T], x_hbm[:, X_FIRST:T])
         load_w1(1, 1)
         load_w1(2, 2)
-        spread_rows(rows_first, x_planes[0], ROWS - 1)
-        spread_s1()
-        x_planes.append(sbuf([P, (E * C - PAIR) // 4], I32, "x_plane_second", offset=E * N))
-        spread_rows(rows_second, x_planes[1])
-        load_s2()
+        spread_rows(rows_first, x_plane_first, ROWS - 1)
+        for r in range(ROWS):
+            nc.sync.dma_start(s1_plane[r:P:QUAD, :, :], s1_turned[r:P:ROWS, :])
+        x_plane_rest = sbuf([P, (E * C - PAIR) // 4], I32, "x_plane_rest", offset=E * N)
+        spread_rows(rows_rest, x_plane_rest)
+        for r in range(ROWS):
+            nc.sync.dma_start(s2_plane[r:P:QUAD, :, :], s2_hbm[r : K // 32 : ROWS, :, :])
         load_w1(4, 2)
         load_w2(0, 2)
         load_w1(6, 2)
         load_w2(2, 2)
         load_w2(4, 4)
+
         gather(0, 1, "w1_raw0")
-        permute(1, nc.scalar.copy)
-        permute(2, nc.scalar.copy)
+        permute(1, on_scalar)
+        permute(2, on_scalar)
         gather(1, 1)
         gather(2, 2)
-        layer1(0, 0)
-        layer1(0, 1)
-        layer1(1, 0)
-        layer1(1, 1)
+        for e in range(2):
+            for m in range(RANKS):
+                layer1(e, m)
         quantise_part(0)
-        layer1_rank(1, 0)
+        layer1_part(2)
         quantise_part(1, "codes")
-        layer1_rank(1, 1)
-        permute(4, nc.vector.tensor_copy)
-        layer2(0)
-        layer2(1)
-        store(0)
+        layer1_part(3)
+        permute(4, on_vector)
+        layer2_part(0)
+        layer2_part(1)
+        store_part(0, on_vector)
         quantise_part(2, "codes")
-        layer2(2)
-        layer1_rank(2, 0)
+        layer2_part(2)
+        layer1_part(4)
         quantise_part(3, "codes")
-        layer2(3)
-        layer1_rank(2, 1)
-        permute(6, nc.vector.tensor_copy)
-        store(1)
+        layer2_part(3)
+        layer1_part(5)
+        permute(6, on_vector)
+        store_part(1, on_vector)
         quantise_part(4)
-        store(2)
-        layer1_rank(3, 0)
-        layer2(4)
+        store_part(2, on_vector)
+        layer1_part(6)
+        layer2_part(4)
         quantise_part(5)
-        store(3)
-        layer1_rank(3, 1)
-        layer2(5)
-        quantise_half(6, 0)
-        quantise_half(7, 0)
-        layer2_half(6, 0, 1)
-        layer2_half(7, 0, 4)
-        quantise_half(6, 1)
-        quantise_half(7, 1)
-        layer2_half(6, 1, 2)
-        store(4)
-        store(5, True)
-        store_half(6, 0, False)
-        store_half(7, 0, False)
-        store_half(6, 1, True)
-        last()
+        store_part(3, on_vector)
+        layer1_part(7)
+        layer2_part(5)
+        last_pair = (E - 2, E - 1)
+        for e in last_pair:
+            quantise_half(e, 0)
+        for e in last_pair:
+            layer2_half(e, 0)
+        for e in last_pair:
+            quantise_half(e, 1)
+        layer2_half(E - 2, 1)
+        store_part(4, on_vector)
+        store_part(5, on_scalar)
+        for e in last_pair:
+            store_half(e, 0, on_vector)
+        store_half(E - 2, 1, on_scalar)
+        h_words, h_plane = codes[E - 1, 1]
+        for g, (copy, queue) in enumerate(((on_vector, nc.sync), (on_scalar, nc.scalar))):
+            y = bank(BANKS // 2 + g, [P, U], "y")
+            staged = sbuf([P, U], F32, "staged_last%d" % g)
+            product2(E - 1, g, h_words, h_plane, y[:])
+            copy(staged[:], y[:])
+            queue.dma_start(out_blocks[g, :, 1, (E - 1) * U : E * U], staged[:])

@@ -24,8 +24,20 @@ PAIR = 2 * C
 ROW0 = P - K // 32
 X_FIRST = 7 * T // 8
 LINE = 8
-BANKS = 8
+RING = 4
+KB = 1024
 FLOPS = 2 * E * C * (K * H + H * N)
+
+AT_X_ROWS = 0
+AT_S1_RAW = 4 * KB
+AT_RAW0 = AT_S1_RAW + 3 * KB // 2
+AT_RAW1 = AT_RAW0 + KB
+AT_RAW2 = AT_RAW1 + 4 * KB
+AT_RAW4 = AT_RAW2 + 2 * KB
+AT_HIDDEN1 = AT_RAW4 + 2 * KB
+AT_RAW6 = AT_HIDDEN1 + 4 * KB
+AT_HIDDEN3 = AT_RAW6 + 2 * KB
+AT_HIDDEN_LAST = AT_HIDDEN3 + 2 * KB
 
 
 def tile_moe_pke_mlp_silu_kernel(
@@ -40,20 +52,20 @@ def tile_moe_pke_mlp_silu_kernel(
         def bank(number, shape, name):
             return psum.tile(shape, F32, name=name, tag="bank%d" % number)
 
-        def sbuf(shape, dtype, name, tag=None, offset=None):
+        def sbuf(shape, dtype, name, offset=None):
             if offset is not None:
                 return turns.tile(shape, dtype, name=name, offset=offset, align_bytes=64)
-            return keep.tile(shape, dtype, name=name, tag=tag or name, align_bytes=64)
+            return keep.tile(shape, dtype, name=name, align_bytes=64)
 
         offsets = keep.tile([P, E * C // 16], U16, name="offsets")
         x_all = sbuf([P, T], I32, "x_all")
-        x_rows = sbuf([P, T // 4], I32, "x_rows", offset=0)
-        s1_raw = sbuf([P, H // 4], I32, "s1_raw")
+        x_rows = sbuf([P, T // 4], I32, "x_rows", AT_X_ROWS)
+        s1_raw = sbuf([P, H // 4], I32, "s1_raw", AT_S1_RAW)
         s1_turned = sbuf([P, H // 4], I32, "s1_turned")
         s1_plane = sbuf([P, E, H // 4], I32, "s1_plane")
         warm_in = keep.tile([P, 1], F32, name="warm_in")
         warm_out = keep.tile([P, 1], F32, name="warm_out")
-        s2_plane = sbuf([P, E, N // 4], I32, "s2_plane", offset=0)
+        s2_plane = sbuf([P, E, N // 4], I32, "s2_plane", AT_X_ROWS)
 
         x_hbm = x_words[0].rearrange("p t r -> p (t r)").bitcast(I32)
         w1_hbm = w1_words.rearrange("e s p b -> p (e s) b").bitcast(I32)
@@ -61,12 +73,15 @@ def tile_moe_pke_mlp_silu_kernel(
         s2_hbm = w2_scales.rearrange("e s q i -> q (e s) i").bitcast(I32)
         out_blocks = out.rearrange("(g p) (m c) -> g p m c", p=P, m=RANKS)
         w1_raw, w1_turned, w2, slot_words, hidden, codes, sums = {}, {}, {}, {}, {}, {}, {}
-        a_banks = [n if n < BANKS else BANKS // 2 + n % (BANKS // 2) for n in range(E * RANKS)]
-        y_banks = [n % (BANKS // 2) for n in range(E * RANKS)]
+        a_banks = [n if n < 2 * RING else n % RING for n in range(E * RANKS)]
+        y_banks = [RING + n % RING for n in range(E)]
 
-        def load_w1(first, count):
-            w1_raw[first] = sbuf([P, count, H // 2], I32, "w1_raw%d" % first)
-            nc.sync.dma_start(w1_raw[first][:], w1_hbm[:, first : first + count, :])
+        def load_w1(first, count, offset):
+            raw = sbuf([P, count, H // 2], I32, "w1_raw%d" % first, offset)
+            nc.sync.dma_start(raw[:], w1_hbm[:, first : first + count, :])
+            for j in range(count):
+                w1_raw[first + j, 1] = raw[:, j : j + 1, :]
+            w1_raw[first, count] = raw[:]
 
         def load_w2(first, count):
             words = sbuf([P, count, N // 2], I32, "w2_%d" % first)
@@ -74,12 +89,11 @@ def tile_moe_pke_mlp_silu_kernel(
             for j in range(count):
                 w2[first + j] = words[:, j, :]
 
-        def permute(first, copy):
-            count = w1_raw[first].shape[1]
+        def permute(first, count, copy):
             turned = sbuf([P, PACK, count, P // 2], I32, "w1_turned%d" % first)
             copy(
                 turned[:].bitcast(U16).rearrange("p t e (a b) -> p (e a) t b", b=LINE),
-                w1_raw[first][:].bitcast(U16).rearrange("p e (a b t) -> p (e a) t b", b=LINE, t=PACK),
+                w1_raw[first, count].bitcast(U16).rearrange("p e (a b t) -> p (e a) t b", b=LINE, t=PACK),
             )
             for j in range(count):
                 w1_turned[first + j] = turned[:, :, j, :]
@@ -87,27 +101,23 @@ def tile_moe_pke_mlp_silu_kernel(
         def list_piece(first, count):
             return offsets[:, first // 16 : (first + count) // 16]
 
-        def gather_rows(first, count, name):
-            rows = sbuf([P, count], U8, name)
+        def gather_rows(first, count, name, offset=None):
+            rows = sbuf([P, count], U8, name, offset)
             nc.vector.tensor_copy(rows[:], x_rows[:].bitcast(U8).indirect(list_piece(first, count)))
             return rows
 
-        def spread_rows(rows, plane, first=0, last=ROWS):
-            for r in range(first, last):
+        def spread_rows(rows, plane):
+            for r in range(ROWS):
                 nc.sync.dma_start(plane[r:P:QUAD, :], rows[ROW0 + r : P : ROWS, :].bitcast(I32))
 
-        def gather(pair, count, tag=None):
-            words = sbuf([P, count * PAIR], U32, "words%d" % pair, tag)
-            nc.vector.tensor_copy(words[:], x_all[:].bitcast(U32).indirect(list_piece(pair * PAIR, count * PAIR)))
+        def gather(first, count, offset=None):
+            words = sbuf([P, count * C], U32, "words%d" % first, offset)
+            nc.vector.tensor_copy(words[:], x_all[:].bitcast(U32).indirect(list_piece(first * C, count * C)))
             for j in range(count):
-                slot_words[pair + j] = words[:, j * PAIR : (j + 1) * PAIR]
+                slot_words[first + j] = words[:, j * C : (j + 1) * C]
 
         def layer1(e, m):
-            part = e // 2 * RANKS + m
-            if part not in hidden:
-                hidden[part] = sbuf([P, 2, U, PACK], BF16, "h%d" % part)
             w1_plane = s1_turned[:] if e == 0 else s1_plane[:, e, :]
-            in_pair = (e % 2) * C + m * U
             slot = e * C + m * U
             if slot < PAIR:
                 x_scale = x_plane_first[:, slot // 4 : (slot + U) // 4]
@@ -119,27 +129,31 @@ def tile_moe_pke_mlp_silu_kernel(
                     out=a[:, t, :],
                     lhsT=w1_turned[e][:, t, :].bitcast(FP4X4),
                     lhsT_scale=w1_plane[:, t * P // 4 : (t + 1) * P // 4].bitcast(U8),
-                    rhs=slot_words[e // 2][:, in_pair : in_pair + U].bitcast(FP8X4),
+                    rhs=slot_words[e][:, m * U : (m + 1) * U].bitcast(FP8X4),
                     rhs_scale=x_scale.bitcast(U8),
                     start=True,
                     stop=True,
                 )
-            nc.scalar.activation(hidden[part][:, e % 2, :, :], a[:].rearrange("p t u -> p u t"), SILU)
+            nc.scalar.activation(hidden[e, m], a[:].rearrange("p t u -> p u t"), SILU)
 
-        def layer1_part(part):
-            pair, m = divmod(part, RANKS)
-            layer1(2 * pair, m)
-            layer1(2 * pair + 1, m)
+        def new_hidden(name, halves, offset=None):
+            tile = sbuf([P, len(halves), U, PACK], BF16, name, offset)
+            for n, half in enumerate(halves):
+                hidden[half] = tile[:, n, :, :]
+            return tile
 
-        def quantise(values, width, name, tag=None):
-            h_words = sbuf([P, width], U32, name, tag)
-            h_plane = sbuf([P, width], U8, name + "_plane")
+        def quantise(tile, halves, name, plane_offset=None, tag=None):
+            width = len(halves) * U
+            h_words = keep.tile([P, width], U32, name=name, tag=tag or name, align_bytes=64)
+            h_plane = sbuf([P, width], U8, name + "_plane", plane_offset)
             nc.vector.quantize_mx(
-                out=h_words[:].bitcast(FP8X4), scales=h_plane[:], in_=values.rearrange("p c t -> p (c t)")
+                out=h_words[:].bitcast(FP8X4), scales=h_plane[:], in_=tile[:].rearrange("p n u t -> p (n u t)")
             )
-            return h_words[:], h_plane[:]
+            for n, half in enumerate(halves):
+                codes[half] = (h_words[:, n * U : (n + 1) * U], h_plane[:, n * U : (n + 1) * U])
 
-        def product2(e, g, h_words, h_plane, y):
+        def product2(e, m, g, y):
+            h_words, h_plane = codes[e, m]
             nc.tensor.matmul_mx(
                 out=y,
                 lhsT=w2[e][:, g * P // 2 : (g + 1) * P // 2].bitcast(FP4X4),
@@ -150,36 +164,20 @@ def tile_moe_pke_mlp_silu_kernel(
                 stop=True,
             )
 
-        def quantise_part(part, tag=None):
-            codes[part] = quantise(hidden[part][:].rearrange("p j u t -> p (j u) t"), C, "h_words%d" % part, tag)
-
-        def layer2_part(part):
-            h_words, h_plane = codes[part]
-            sums[part] = bank(y_banks.pop(0), [P, G, 2, U], "y")
-            for j in range(2):
-                cols = slice(j * U, (j + 1) * U)
+        def layer2(first, count, m):
+            sums[first, m] = bank(y_banks.pop(0), [P, G, count, U], "y")
+            for j in range(count):
                 for g in range(G):
-                    product2(part // RANKS * 2 + j, g, h_words[:, cols], h_plane[:, cols], sums[part][:, g, j, :])
+                    product2(first + j, m, g, sums[first, m][:, g, j, :])
 
-        def store_part(part, copy):
-            pair, m = divmod(part, RANKS)
-            staged = sbuf([P, G, C], F32, "staged%d" % part)
-            copy(staged[:], sums[part][:].rearrange("p g j u -> p g (j u)"))
-            nc.sync.dma_start(out_blocks[:, :, m, pair * C : (pair + 1) * C].rearrange("g p c -> p g c"), staged[:])
+        def store(first, count, m, copy, offset=None):
+            staged = sbuf([P, G, count * U], F32, "staged%d_%d" % (first, m), offset)
+            copy(staged[:], sums[first, m][:].rearrange("p g j u -> p g (j u)"))
+            columns = slice(first * U, (first + count) * U)
+            nc.sync.dma_start(out_blocks[:, :, m, columns].rearrange("g p c -> p g c"), staged[:])
 
-        def quantise_half(e, m):
-            codes[e, m] = quantise(hidden[e // 2 * RANKS + m][:, e % 2, :, :], U, "h_words%d_%d" % (e, m))
-
-        def layer2_half(e, m):
-            h_words, h_plane = codes[e, m]
-            sums[e, m] = bank(y_banks.pop(0), [P, G, U], "y")
-            for g in range(G):
-                product2(e, g, h_words, h_plane, sums[e, m][:, g, :])
-
-        def store_half(e, m, copy):
-            staged = sbuf([P, G, U], F32, "staged%d_%d" % (e, m))
-            copy(staged[:], sums[e, m][:])
-            nc.sync.dma_start(out_blocks[:, :, m, e * U : (e + 1) * U].rearrange("g p u -> p g u"), staged[:])
+        def pair_halves(first):
+            return [(first + j, m) for m in range(RANKS) for j in range(2)]
 
         on_vector, on_scalar = nc.vector.tensor_copy, nc.scalar.copy
 
@@ -192,7 +190,7 @@ def tile_moe_pke_mlp_silu_kernel(
             )
         nc.sync.dma_start(x_rows[ROW0:P, :], x_scales[0].bitcast(I32))
         nc.sync.dma_start(offsets[:], offs)
-        load_w1(0, 1)
+        load_w1(0, 1, AT_RAW0)
         nc.sync.dma_start(x_all[:, 0:X_FIRST], x_hbm[:, 0:X_FIRST])
         nc.scalar.activation(warm_out[:], warm_in[:], SILU)
 
@@ -201,75 +199,83 @@ def tile_moe_pke_mlp_silu_kernel(
             s1_raw[:].bitcast(U8).rearrange("p (m t) -> p t m", t=PACK),
         )
         rows_first = gather_rows(0, PAIR, "rows_first")
-        permute(0, on_scalar)
+        permute(0, 1, on_scalar)
         rows_rest = gather_rows(PAIR, E * C - PAIR, "rows_rest")
-        x_plane_first = sbuf([P, PAIR // 4], I32, "x_plane_first", "s1_raw")
-        spread_rows(rows_first, x_plane_first, 0, ROWS - 1)
+        x_plane_first = sbuf([P, PAIR // 4], I32, "x_plane_first", AT_S1_RAW)
+        spread_rows(rows_first, x_plane_first)
         nc.sync.dma_start(x_all[:, X_FIRST:T], x_hbm[:, X_FIRST:T])
-        load_w1(1, 1)
-        load_w1(2, 2)
-        spread_rows(rows_first, x_plane_first, ROWS - 1)
+        load_w1(1, 1, AT_RAW1)
+        load_w1(2, 2, AT_RAW2)
         for r in range(ROWS):
             nc.sync.dma_start(s1_plane[r:P:QUAD, :, :], s1_turned[r:P:ROWS, :])
-        x_plane_rest = sbuf([P, (E * C - PAIR) // 4], I32, "x_plane_rest", offset=E * N)
+        load_w1(4, 2, AT_RAW4)
+        x_plane_rest = sbuf([P, (E * C - PAIR) // 4], I32, "x_plane_rest", AT_X_ROWS + E * N)
         spread_rows(rows_rest, x_plane_rest)
+        load_w2(0, 4)
         for r in range(ROWS):
             nc.sync.dma_start(s2_plane[r:P:QUAD, :, :], s2_hbm[r : K // 32 : ROWS, :, :])
-        load_w1(4, 2)
-        load_w2(0, 2)
-        load_w1(6, 2)
-        load_w2(2, 2)
+        load_w1(6, 2, AT_RAW6)
         load_w2(4, 4)
 
-        gather(0, 1, "w1_raw0")
-        permute(1, on_scalar)
-        permute(2, on_scalar)
+        on_gpsimd = nc.gpsimd.tensor_copy
+        parts = [[(2 * pair, m), (2 * pair + 1, m)] for pair in range(E // 2) for m in range(RANKS)]
+        tiles = {}
+
+        def layer1_part(part):
+            tiles[part] = new_hidden("hidden%d" % part, parts[part])
+            for half in parts[part]:
+                layer1(*half)
+
+        def quantise_part(part):
+            quantise(tiles[part], parts[part], "codes%d" % part, tag="codes_ring%d" % (part % 3))
+            layer2(parts[part][0][0], 2, part % RANKS)
+
+        def store_part(part, copy):
+            store(parts[part][0][0], 2, part % RANKS, copy)
+
+        gather(0, 1, AT_RAW0)
+        permute(1, 1, on_scalar)
         gather(1, 1)
         gather(2, 2)
+        gather(4, 2)
+        gather(6, 2)
+        permute(2, 1, on_gpsimd)
+        permute(3, 1, on_gpsimd)
+        permute(4, 2, on_gpsimd)
+        permute(6, 2, on_gpsimd)
+        tiles[0] = new_hidden("hidden0", parts[0], AT_RAW1)
+        tiles[1] = new_hidden("hidden1", parts[1])
         for e in range(2):
             for m in range(RANKS):
                 layer1(e, m)
+        for part in range(2, 6):
+            layer1_part(part)
         quantise_part(0)
-        layer1_part(2)
-        quantise_part(1, "codes")
-        layer1_part(3)
-        permute(4, on_vector)
-        layer2_part(0)
-        layer2_part(1)
+        quantise_part(1)
+        quantise_part(2)
+        quantise_part(3)
         store_part(0, on_vector)
-        quantise_part(2, "codes")
-        layer2_part(2)
-        layer1_part(4)
-        quantise_part(3, "codes")
-        layer2_part(3)
-        layer1_part(5)
-        permute(6, on_vector)
+        layer1_part(6)
+        hidden14 = new_hidden("hidden14", [(6, 1)])
+        layer1(6, 1)
+        hidden15 = new_hidden("hidden15", [(7, 1)])
+        layer1(7, 1)
         store_part(1, on_vector)
         quantise_part(4)
         store_part(2, on_vector)
-        layer1_part(6)
-        layer2_part(4)
         quantise_part(5)
         store_part(3, on_vector)
-        layer1_part(7)
-        layer2_part(5)
-        last_pair = (E - 2, E - 1)
-        for e in last_pair:
-            quantise_half(e, 0)
-        for e in last_pair:
-            layer2_half(e, 0)
-        for e in last_pair:
-            quantise_half(e, 1)
-        layer2_half(E - 2, 1)
+        quantise_part(6)
         store_part(4, on_vector)
+        quantise(hidden14, [(6, 1)], "codes14")
+        layer2(6, 1, 1)
+        quantise(hidden15, [(7, 1)], "codes15")
         store_part(5, on_scalar)
-        for e in last_pair:
-            store_half(e, 0, on_vector)
-        store_half(E - 2, 1, on_scalar)
-        h_words, h_plane = codes[E - 1, 1]
+        store_part(6, on_vector)
+        store(6, 1, 1, on_scalar)
         for g, (copy, queue) in enumerate(((on_vector, nc.sync), (on_scalar, nc.scalar))):
-            y = bank(BANKS // 2 + g, [P, U], "y")
+            y = bank(g, [P, U], "y")
             staged = sbuf([P, U], F32, "staged_last%d" % g)
-            product2(E - 1, g, h_words, h_plane, y[:])
+            product2(E - 1, 1, g, y[:])
             copy(staged[:], y[:])
             queue.dma_start(out_blocks[g, :, 1, (E - 1) * U : E * U], staged[:])

@@ -63,6 +63,7 @@ def tile_moe_pke_mlp_silu_kernel(
         s1_raw = sbuf([P, H // 4], I32, "s1_raw", AT_S1_RAW)
         s1_turned = sbuf([P, H // 4], I32, "s1_turned")
         s1_plane = sbuf([P, E, H // 4], I32, "s1_plane")
+        x_plane_first = sbuf([P, PAIR // 4], I32, "x_plane_first")
         warm_in = keep.tile([P, 1], F32, name="warm_in")
         warm_out = keep.tile([P, 1], F32, name="warm_out")
         s2_plane = sbuf([P, E, N // 4], I32, "s2_plane", AT_X_ROWS)
@@ -76,7 +77,7 @@ def tile_moe_pke_mlp_silu_kernel(
         a_banks = [n if n < 2 * RING else n % RING for n in range(E * RANKS)]
         y_banks = [RING + n % RING for n in range(E)]
 
-        def load_w1(first, count, offset):
+        def load_w1(first, count, offset=None):
             raw = sbuf([P, count, H // 2], I32, "w1_raw%d" % first, offset)
             nc.sync.dma_start(raw[:], w1_hbm[:, first : first + count, :])
             for j in range(count):
@@ -89,12 +90,13 @@ def tile_moe_pke_mlp_silu_kernel(
             for j in range(count):
                 w2[first + j] = words[:, j, :]
 
-        def permute(first, count, copy):
+        def permute(first, count, *copies):
             turned = sbuf([P, PACK, count, P // 2], I32, "w1_turned%d" % first)
-            copy(
-                turned[:].bitcast(U16).rearrange("p t e (a b) -> p (e a) t b", b=LINE),
-                w1_raw[first, count].bitcast(U16).rearrange("p e (a b t) -> p (e a) t b", b=LINE, t=PACK),
-            )
+            to = turned[:].bitcast(U16).rearrange("p t e (a b) -> p (e a) t b", b=LINE)
+            source = w1_raw[first, count].bitcast(U16).rearrange("p e (a b t) -> p (e a) t b", b=LINE, t=PACK)
+            share = PACK // len(copies)
+            for n, copy in enumerate(copies):
+                copy(to[:, :, n * share : (n + 1) * share, :], source[:, :, n * share : (n + 1) * share, :])
             for j in range(count):
                 w1_turned[first + j] = turned[:, :, j, :]
 
@@ -183,38 +185,36 @@ def tile_moe_pke_mlp_silu_kernel(
 
         nc.vector.memset(warm_in[:], 0.0)
         nc.vector.memset(x_rows[0:ROW0, :], 0)
-        nc.vector.memset(s1_plane[:], 0)
+        nc.gpsimd.memset(x_plane_first[:], 0)
+        nc.gpsimd.memset(s1_plane[:], 0)
+        nc.sync.dma_start(x_rows[ROW0:P, :], x_scales[0].bitcast(I32))
+        nc.sync.dma_start(offsets[:], offs)
         for q, queue in enumerate((nc.sync, nc.sync, nc.scalar, nc.scalar)):
             queue.dma_start(
                 s1_raw[QUAD * q : QUAD * (q + 1), :], w1_scales[:, 0, ROWS * q : ROWS * (q + 1), :].bitcast(I32)
             )
-        nc.sync.dma_start(x_rows[ROW0:P, :], x_scales[0].bitcast(I32))
-        nc.sync.dma_start(offsets[:], offs)
-        load_w1(0, 1, AT_RAW0)
         nc.sync.dma_start(x_all[:, 0:X_FIRST], x_hbm[:, 0:X_FIRST])
         nc.scalar.activation(warm_out[:], warm_in[:], SILU)
 
-        nc.vector.tensor_copy(
+        nc.gpsimd.tensor_copy(
             s1_turned[:].bitcast(U8).rearrange("p (t m) -> p t m", t=PACK),
             s1_raw[:].bitcast(U8).rearrange("p (m t) -> p t m", t=PACK),
         )
         rows_first = gather_rows(0, PAIR, "rows_first")
-        permute(0, 1, on_scalar)
-        rows_rest = gather_rows(PAIR, E * C - PAIR, "rows_rest")
-        x_plane_first = sbuf([P, PAIR // 4], I32, "x_plane_first", AT_S1_RAW)
+        rows_rest = gather_rows(PAIR, E * C - PAIR, "rows_rest", AT_S1_RAW)
         spread_rows(rows_first, x_plane_first)
         nc.sync.dma_start(x_all[:, X_FIRST:T], x_hbm[:, X_FIRST:T])
-        load_w1(1, 1, AT_RAW1)
-        load_w1(2, 2, AT_RAW2)
+        load_w1(0, 1)
+        load_w1(1, 3, AT_RAW1)
         for r in range(ROWS):
             nc.sync.dma_start(s1_plane[r:P:QUAD, :, :], s1_turned[r:P:ROWS, :])
-        load_w1(4, 2, AT_RAW4)
+        load_w1(4, 2)
         x_plane_rest = sbuf([P, (E * C - PAIR) // 4], I32, "x_plane_rest", AT_X_ROWS + E * N)
         spread_rows(rows_rest, x_plane_rest)
         load_w2(0, 4)
         for r in range(ROWS):
             nc.sync.dma_start(s2_plane[r:P:QUAD, :, :], s2_hbm[r : K // 32 : ROWS, :, :])
-        load_w1(6, 2, AT_RAW6)
+        load_w1(6, 2)
         load_w2(4, 4)
 
         on_gpsimd = nc.gpsimd.tensor_copy
@@ -227,13 +227,14 @@ def tile_moe_pke_mlp_silu_kernel(
                 layer1(*half)
 
         def quantise_part(part):
-            quantise(tiles[part], parts[part], "codes%d" % part, tag="codes_ring%d" % (part % 3))
+            quantise(tiles[part], parts[part], "codes%d" % part, tag="codes_ring%d" % (part % 2) if part else None)
             layer2(parts[part][0][0], 2, part % RANKS)
 
         def store_part(part, copy):
             store(parts[part][0][0], 2, part % RANKS, copy)
 
-        gather(0, 1, AT_RAW0)
+        gather(0, 1)
+        permute(0, 1, on_scalar, on_gpsimd)
         permute(1, 1, on_scalar)
         gather(1, 1)
         gather(2, 2)
@@ -243,7 +244,7 @@ def tile_moe_pke_mlp_silu_kernel(
         permute(3, 1, on_gpsimd)
         permute(4, 2, on_gpsimd)
         permute(6, 2, on_gpsimd)
-        tiles[0] = new_hidden("hidden0", parts[0], AT_RAW1)
+        tiles[0] = new_hidden("hidden0", parts[0])
         tiles[1] = new_hidden("hidden1", parts[1])
         for e in range(2):
             for m in range(RANKS):
@@ -253,20 +254,20 @@ def tile_moe_pke_mlp_silu_kernel(
         quantise_part(0)
         quantise_part(1)
         quantise_part(2)
-        quantise_part(3)
         store_part(0, on_vector)
+        quantise_part(3)
         layer1_part(6)
         hidden14 = new_hidden("hidden14", [(6, 1)])
         layer1(6, 1)
         hidden15 = new_hidden("hidden15", [(7, 1)])
         layer1(7, 1)
         store_part(1, on_vector)
-        quantise_part(4)
         store_part(2, on_vector)
-        quantise_part(5)
+        quantise_part(4)
         store_part(3, on_vector)
-        quantise_part(6)
+        quantise_part(5)
         store_part(4, on_vector)
+        quantise_part(6)
         quantise(hidden14, [(6, 1)], "codes14")
         layer2(6, 1, 1)
         quantise(hidden15, [(7, 1)], "codes15")

@@ -74,15 +74,16 @@ def tile_moe_pke_mlp_silu_kernel(
         s2_hbm = w2_scales.rearrange("e s q i -> q (e s) i").bitcast(I32)
         out_blocks = out.rearrange("(g p) (m c) -> g p m c", p=P, m=RANKS)
         w1_raw, w1_turned, w2, slot_words, hidden, codes, sums = {}, {}, {}, {}, {}, {}, {}
-        a_banks = [n if n < 2 * RING else n % RING for n in range(E * RANKS)]
-        y_banks = [RING + n % RING for n in range(E)]
+        a_banks = [n % (2 * RING) if n < 3 * RING else RING + n % RING for n in range(E * RANKS)]
+        y_banks = [(RING + n) % (2 * RING) for n in range(E)]
 
         def load_w1(first, count, offset=None):
             raw = sbuf([P, count, H // 2], I32, "w1_raw%d" % first, offset)
             nc.sync.dma_start(raw[:], w1_hbm[:, first : first + count, :])
             for j in range(count):
                 w1_raw[first + j, 1] = raw[:, j : j + 1, :]
-            w1_raw[first, count] = raw[:]
+            for j in range(count - 1):
+                w1_raw[first + j, 2] = raw[:, j : j + 2, :]
 
         def load_w2(first, count):
             words = sbuf([P, count, N // 2], I32, "w2_%d" % first)
@@ -90,8 +91,8 @@ def tile_moe_pke_mlp_silu_kernel(
             for j in range(count):
                 w2[first + j] = words[:, j, :]
 
-        def permute(first, count, *copies):
-            turned = sbuf([P, PACK, count, P // 2], I32, "w1_turned%d" % first)
+        def permute(first, count, *copies, offset=None):
+            turned = sbuf([P, PACK, count, P // 2], I32, "w1_turned%d" % first, offset)
             to = turned[:].bitcast(U16).rearrange("p t e (a b) -> p (e a) t b", b=LINE)
             source = w1_raw[first, count].bitcast(U16).rearrange("p e (a b t) -> p (e a) t b", b=LINE, t=PACK)
             share = PACK // len(copies)
@@ -201,7 +202,7 @@ def tile_moe_pke_mlp_silu_kernel(
             s1_raw[:].bitcast(U8).rearrange("p (m t) -> p t m", t=PACK),
         )
         rows_first = gather_rows(0, PAIR, "rows_first")
-        rows_rest = gather_rows(PAIR, E * C - PAIR, "rows_rest", AT_S1_RAW)
+        rows_rest = gather_rows(PAIR, E * C - PAIR, "rows_rest")
         spread_rows(rows_first, x_plane_first)
         nc.sync.dma_start(x_all[:, X_FIRST:T], x_hbm[:, X_FIRST:T])
         load_w1(0, 1)
@@ -211,10 +212,10 @@ def tile_moe_pke_mlp_silu_kernel(
         load_w1(4, 2)
         x_plane_rest = sbuf([P, (E * C - PAIR) // 4], I32, "x_plane_rest", AT_X_ROWS + E * N)
         spread_rows(rows_rest, x_plane_rest)
+        load_w1(6, 2)
         load_w2(0, 4)
         for r in range(ROWS):
             nc.sync.dma_start(s2_plane[r:P:QUAD, :, :], s2_hbm[r : K // 32 : ROWS, :, :])
-        load_w1(6, 2)
         load_w2(4, 4)
 
         on_gpsimd = nc.gpsimd.tensor_copy
@@ -234,14 +235,13 @@ def tile_moe_pke_mlp_silu_kernel(
             store(parts[part][0][0], 2, part % RANKS, copy)
 
         gather(0, 1)
-        permute(0, 1, on_scalar, on_gpsimd)
+        permute(0, 1, on_scalar, on_gpsimd, offset=AT_S1_RAW)
         permute(1, 1, on_scalar)
         gather(1, 1)
         gather(2, 2)
         gather(4, 2)
         gather(6, 2)
-        permute(2, 1, on_gpsimd)
-        permute(3, 1, on_gpsimd)
+        permute(2, 2, on_gpsimd)
         permute(4, 2, on_gpsimd)
         permute(6, 2, on_gpsimd)
         tiles[0] = new_hidden("hidden0", parts[0])
@@ -256,15 +256,15 @@ def tile_moe_pke_mlp_silu_kernel(
         quantise_part(2)
         store_part(0, on_vector)
         quantise_part(3)
+        store_part(1, on_vector)
+        store_part(2, on_vector)
         layer1_part(6)
         hidden14 = new_hidden("hidden14", [(6, 1)])
         layer1(6, 1)
-        hidden15 = new_hidden("hidden15", [(7, 1)])
-        layer1(7, 1)
-        store_part(1, on_vector)
-        store_part(2, on_vector)
         quantise_part(4)
         store_part(3, on_vector)
+        hidden15 = new_hidden("hidden15", [(7, 1)])
+        layer1(7, 1)
         quantise_part(5)
         store_part(4, on_vector)
         quantise_part(6)
@@ -275,7 +275,7 @@ def tile_moe_pke_mlp_silu_kernel(
         store_part(6, on_vector)
         store(6, 1, 1, on_scalar)
         for g, (copy, queue) in enumerate(((on_vector, nc.sync), (on_scalar, nc.scalar))):
-            y = bank(g, [P, U], "y")
+            y = bank(RING + g, [P, U], "y")
             staged = sbuf([P, U], F32, "staged_last%d" % g)
             product2(E - 1, 1, g, y[:])
             copy(staged[:], y[:])

@@ -91,13 +91,17 @@ def tile_moe_pke_mlp_silu_kernel(
             for j in range(count):
                 w2[first + j] = words[:, j, :]
 
-        def permute(first, count, *copies, offset=None):
+        def permute(first, count, scalar_share=0, offset=None):
             turned = sbuf([P, PACK, count, P // 2], I32, "w1_turned%d" % first, offset)
             to = turned[:].bitcast(U16).rearrange("p t e (a b) -> p (e a) t b", b=LINE)
             source = w1_raw[first, count].bitcast(U16).rearrange("p e (a b t) -> p (e a) t b", b=LINE, t=PACK)
-            share = PACK // len(copies)
-            for n, copy in enumerate(copies):
-                copy(to[:, :, n * share : (n + 1) * share, :], source[:, :, n * share : (n + 1) * share, :])
+            long_to = turned[:].bitcast(U16)
+            long_source = w1_raw[first, count].bitcast(U16).rearrange("p e (m t) -> p t e m", t=PACK)
+            mine, rest = slice(0, scalar_share), slice(scalar_share, PACK)
+            if scalar_share > 0:
+                nc.scalar.copy(to[:, :, mine, :], source[:, :, mine, :])
+            if scalar_share < PACK:
+                nc.gpsimd.tensor_copy(long_to[:, rest, :, :], long_source[:, rest, :, :])
             for j in range(count):
                 w1_turned[first + j] = turned[:, :, j, :]
 
@@ -218,12 +222,11 @@ def tile_moe_pke_mlp_silu_kernel(
             nc.sync.dma_start(s2_plane[r:P:QUAD, :, :], s2_hbm[r : K // 32 : ROWS, :, :])
         load_w2(4, 4)
 
-        on_gpsimd = nc.gpsimd.tensor_copy
         parts = [[(2 * pair, m), (2 * pair + 1, m)] for pair in range(E // 2) for m in range(RANKS)]
         tiles = {}
 
         def layer1_part(part):
-            tiles[part] = new_hidden("hidden%d" % part, parts[part])
+            tiles[part] = new_hidden("hidden%d" % part, parts[part], AT_HIDDEN3 if part == 3 else None)
             for half in parts[part]:
                 layer1(*half)
 
@@ -235,15 +238,15 @@ def tile_moe_pke_mlp_silu_kernel(
             store(parts[part][0][0], 2, part % RANKS, copy)
 
         gather(0, 1)
-        permute(0, 1, on_scalar, on_gpsimd, offset=AT_S1_RAW)
-        permute(1, 1, on_scalar)
+        permute(0, 1, PACK - 1, AT_S1_RAW)
+        permute(1, 1, PACK)
         gather(1, 1)
         gather(2, 2)
         gather(4, 2)
         gather(6, 2)
-        permute(2, 2, on_gpsimd)
-        permute(4, 2, on_gpsimd)
-        permute(6, 2, on_gpsimd)
+        permute(2, 2)
+        permute(4, 2)
+        permute(6, 1)
         tiles[0] = new_hidden("hidden0", parts[0])
         tiles[1] = new_hidden("hidden1", parts[1])
         for e in range(2):
@@ -256,6 +259,7 @@ def tile_moe_pke_mlp_silu_kernel(
         quantise_part(2)
         store_part(0, on_vector)
         quantise_part(3)
+        permute(7, 1, 0, AT_HIDDEN3)
         store_part(1, on_vector)
         store_part(2, on_vector)
         layer1_part(6)

@@ -91,16 +91,18 @@ def tile_moe_pke_mlp_silu_kernel(
             for j in range(count):
                 w2[first + j] = words[:, j, :]
 
-        def permute(first, count, scalar_share=0, offset=None):
+        def permute(first, count, scalar_share=0, offset=None, vector=False):
             turned = sbuf([P, PACK, count, P // 2], I32, "w1_turned%d" % first, offset)
             to = turned[:].bitcast(U16).rearrange("p t e (a b) -> p (e a) t b", b=LINE)
             source = w1_raw[first, count].bitcast(U16).rearrange("p e (a b t) -> p (e a) t b", b=LINE, t=PACK)
             long_to = turned[:].bitcast(U16)
             long_source = w1_raw[first, count].bitcast(U16).rearrange("p e (m t) -> p t e m", t=PACK)
             mine, rest = slice(0, scalar_share), slice(scalar_share, PACK)
-            if scalar_share > 0:
+            if vector:
+                nc.vector.tensor_copy(to, source)
+            elif scalar_share > 0:
                 nc.scalar.copy(to[:, :, mine, :], source[:, :, mine, :])
-            if scalar_share < PACK:
+            if scalar_share < PACK and not vector:
                 nc.gpsimd.tensor_copy(long_to[:, rest, :, :], long_source[:, rest, :, :])
             for j in range(count):
                 w1_turned[first + j] = turned[:, :, j, :]
@@ -226,7 +228,7 @@ def tile_moe_pke_mlp_silu_kernel(
         tiles = {}
 
         def layer1_part(part):
-            tiles[part] = new_hidden("hidden%d" % part, parts[part], AT_HIDDEN3 if part == 3 else None)
+            tiles[part] = new_hidden("hidden%d" % part, parts[part], None)
             for half in parts[part]:
                 layer1(*half)
 
@@ -246,7 +248,6 @@ def tile_moe_pke_mlp_silu_kernel(
         gather(6, 2)
         permute(2, 2)
         permute(4, 2)
-        permute(6, 1)
         tiles[0] = new_hidden("hidden0", parts[0])
         tiles[1] = new_hidden("hidden1", parts[1])
         for e in range(2):
@@ -256,10 +257,10 @@ def tile_moe_pke_mlp_silu_kernel(
             layer1_part(part)
         quantise_part(0)
         quantise_part(1)
+        permute(6, 2, vector=True)
         quantise_part(2)
         store_part(0, on_vector)
         quantise_part(3)
-        permute(7, 1, 0, AT_HIDDEN3)
         store_part(1, on_vector)
         store_part(2, on_vector)
         layer1_part(6)

@@ -21,23 +21,13 @@ RANKS = 2
 U = C // RANKS
 G = N // P
 PAIR = 2 * C
+PARTS = E // 2 * RANKS
 ROW0 = P - K // 32
 X_FIRST = 7 * T // 8
 LINE = 8
-RING = 4
-KB = 1024
+BANKS = 8
+SIDE = BANKS // 2
 FLOPS = 2 * E * C * (K * H + H * N)
-
-AT_X_ROWS = 0
-AT_S1_RAW = 4 * KB
-AT_RAW0 = AT_S1_RAW + 3 * KB // 2
-AT_RAW1 = AT_RAW0 + KB
-AT_RAW2 = AT_RAW1 + 4 * KB
-AT_RAW4 = AT_RAW2 + 2 * KB
-AT_HIDDEN1 = AT_RAW4 + 2 * KB
-AT_RAW6 = AT_HIDDEN1 + 4 * KB
-AT_HIDDEN3 = AT_RAW6 + 2 * KB
-AT_HIDDEN_LAST = AT_HIDDEN3 + 2 * KB
 
 
 def tile_moe_pke_mlp_silu_kernel(
@@ -52,38 +42,37 @@ def tile_moe_pke_mlp_silu_kernel(
         def bank(number, shape, name):
             return psum.tile(shape, F32, name=name, tag="bank%d" % number)
 
-        def sbuf(shape, dtype, name, offset=None):
+        def sbuf(shape, dtype, name, tag=None, offset=None):
             if offset is not None:
                 return turns.tile(shape, dtype, name=name, offset=offset, align_bytes=64)
-            return keep.tile(shape, dtype, name=name, align_bytes=64)
+            return keep.tile(shape, dtype, name=name, tag=tag or name, align_bytes=64)
 
         offsets = keep.tile([P, E * C // 16], U16, name="offsets")
         x_all = sbuf([P, T], I32, "x_all")
-        x_rows = sbuf([P, T // 4], I32, "x_rows", AT_X_ROWS)
-        s1_raw = sbuf([P, H // 4], I32, "s1_raw", AT_S1_RAW)
+        x_rows = sbuf([P, T // 4], I32, "x_rows", offset=0)
+        s1_raw = sbuf([P, H // 4], I32, "s1_raw")
         s1_turned = sbuf([P, H // 4], I32, "s1_turned")
         s1_plane = sbuf([P, E, H // 4], I32, "s1_plane")
         x_plane_first = sbuf([P, PAIR // 4], I32, "x_plane_first")
         warm_in = keep.tile([P, 1], F32, name="warm_in")
         warm_out = keep.tile([P, 1], F32, name="warm_out")
-        s2_plane = sbuf([P, E, N // 4], I32, "s2_plane", AT_X_ROWS)
+        s2_plane = sbuf([P, E, N // 4], I32, "s2_plane", offset=0)
 
         x_hbm = x_words[0].rearrange("p t r -> p (t r)").bitcast(I32)
         w1_hbm = w1_words.rearrange("e s p b -> p (e s) b").bitcast(I32)
         w2_hbm = w2_words.rearrange("e s p b -> p (e s) b").bitcast(I32)
         s2_hbm = w2_scales.rearrange("e s q i -> q (e s) i").bitcast(I32)
         out_blocks = out.rearrange("(g p) (m c) -> g p m c", p=P, m=RANKS)
-        w1_raw, w1_turned, w2, slot_words, hidden, codes, sums = {}, {}, {}, {}, {}, {}, {}
-        a_banks = [n % (2 * RING) if n < 3 * RING else RING + n % RING for n in range(E * RANKS)]
-        y_banks = [(RING + n) % (2 * RING) for n in range(E)]
+        w1_loads, w1_turned, w2, slot_words, hidden, hidden_tiles, codes, sums = {}, {}, {}, {}, {}, {}, {}, {}
+        parts = [[(2 * pair, m), (2 * pair + 1, m)] for pair in range(E // 2) for m in range(RANKS)]
+        a_banks = [n % BANKS if n < BANKS + SIDE else SIDE + n % SIDE for n in range(E * RANKS)]
+        y_banks = [(SIDE + n) % BANKS for n in range(PARTS)]
 
-        def load_w1(first, count, offset=None):
-            raw = sbuf([P, count, H // 2], I32, "w1_raw%d" % first, offset)
+        def load_w1(first, count):
+            raw = sbuf([P, count, H // 2], I32, "w1_raw%d" % first)
             nc.sync.dma_start(raw[:], w1_hbm[:, first : first + count, :])
             for j in range(count):
-                w1_raw[first + j, 1] = raw[:, j : j + 1, :]
-            for j in range(count - 1):
-                w1_raw[first + j, 2] = raw[:, j : j + 2, :]
+                w1_loads[first + j] = (raw, j)
 
         def load_w2(first, count):
             words = sbuf([P, count, N // 2], I32, "w2_%d" % first)
@@ -91,27 +80,29 @@ def tile_moe_pke_mlp_silu_kernel(
             for j in range(count):
                 w2[first + j] = words[:, j, :]
 
-        def permute(first, count, scalar_share=0, offset=None, vector=False):
-            turned = sbuf([P, PACK, count, P // 2], I32, "w1_turned%d" % first, offset)
-            to = turned[:].bitcast(U16).rearrange("p t e (a b) -> p (e a) t b", b=LINE)
-            source = w1_raw[first, count].bitcast(U16).rearrange("p e (a b t) -> p (e a) t b", b=LINE, t=PACK)
-            long_to = turned[:].bitcast(U16)
-            long_source = w1_raw[first, count].bitcast(U16).rearrange("p e (m t) -> p t e m", t=PACK)
-            mine, rest = slice(0, scalar_share), slice(scalar_share, PACK)
-            if vector:
-                nc.vector.tensor_copy(to, source)
-            elif scalar_share > 0:
-                nc.scalar.copy(to[:, :, mine, :], source[:, :, mine, :])
-            if scalar_share < PACK and not vector:
-                nc.gpsimd.tensor_copy(long_to[:, rest, :, :], long_source[:, rest, :, :])
+        def permute_views(first, count, tag):
+            raw, at = w1_loads[first]
+            turned = sbuf([P, PACK, count, P // 2], I32, "w1_turned%d" % first, tag)
             for j in range(count):
                 w1_turned[first + j] = turned[:, :, j, :]
+            return turned[:].bitcast(U16), raw[:, at : at + count, :].bitcast(U16)
+
+        def permute(first, count, copy, tag=None):
+            turned, raw = permute_views(first, count, tag)
+            copy(
+                turned.rearrange("p t e (a b) -> p (e a) t b", b=LINE),
+                raw.rearrange("p e (a b t) -> p (e a) t b", b=LINE, t=PACK),
+            )
+
+        def permute_on_gpsimd(first, count):
+            turned, raw = permute_views(first, count, None)
+            nc.gpsimd.tensor_copy(turned, raw.rearrange("p e (m t) -> p t e m", t=PACK))
 
         def list_piece(first, count):
             return offsets[:, first // 16 : (first + count) // 16]
 
-        def gather_rows(first, count, name, offset=None):
-            rows = sbuf([P, count], U8, name, offset)
+        def gather_rows(first, count, name):
+            rows = sbuf([P, count], U8, name)
             nc.vector.tensor_copy(rows[:], x_rows[:].bitcast(U8).indirect(list_piece(first, count)))
             return rows
 
@@ -119,11 +110,17 @@ def tile_moe_pke_mlp_silu_kernel(
             for r in range(ROWS):
                 nc.sync.dma_start(plane[r:P:QUAD, :], rows[ROW0 + r : P : ROWS, :].bitcast(I32))
 
-        def gather(first, count, offset=None):
-            words = sbuf([P, count * C], U32, "words%d" % first, offset)
+        def gather(first, count):
+            words = sbuf([P, count * C], U32, "words%d" % first)
             nc.vector.tensor_copy(words[:], x_all[:].bitcast(U32).indirect(list_piece(first * C, count * C)))
             for j in range(count):
                 slot_words[first + j] = words[:, j * C : (j + 1) * C]
+
+        def new_hidden(name, halves):
+            tile = sbuf([P, len(halves), U, PACK], BF16, name)
+            for n, half in enumerate(halves):
+                hidden[half] = tile[:, n, :, :]
+            return tile
 
         def layer1(e, m):
             w1_plane = s1_turned[:] if e == 0 else s1_plane[:, e, :]
@@ -145,16 +142,15 @@ def tile_moe_pke_mlp_silu_kernel(
                 )
             nc.scalar.activation(hidden[e, m], a[:].rearrange("p t u -> p u t"), SILU)
 
-        def new_hidden(name, halves, offset=None):
-            tile = sbuf([P, len(halves), U, PACK], BF16, name, offset)
-            for n, half in enumerate(halves):
-                hidden[half] = tile[:, n, :, :]
-            return tile
+        def layer1_part(part):
+            hidden_tiles[part] = new_hidden("hidden%d" % part, parts[part])
+            for half in parts[part]:
+                layer1(*half)
 
-        def quantise(tile, halves, name, plane_offset=None, tag=None):
+        def quantise(tile, halves, name, tag=None):
             width = len(halves) * U
-            h_words = keep.tile([P, width], U32, name=name, tag=tag or name, align_bytes=64)
-            h_plane = sbuf([P, width], U8, name + "_plane", plane_offset)
+            h_words = sbuf([P, width], U32, name, tag)
+            h_plane = sbuf([P, width], U8, name + "_plane")
             nc.vector.quantize_mx(
                 out=h_words[:].bitcast(FP8X4), scales=h_plane[:], in_=tile[:].rearrange("p n u t -> p (n u t)")
             )
@@ -173,20 +169,23 @@ def tile_moe_pke_mlp_silu_kernel(
                 stop=True,
             )
 
-        def layer2(first, count, m):
-            sums[first, m] = bank(y_banks.pop(0), [P, G, count, U], "y")
-            for j in range(count):
+        def layer2(halves):
+            sums[halves[0]] = bank(y_banks.pop(0), [P, G, len(halves), U], "y")
+            for j, (e, m) in enumerate(halves):
                 for g in range(G):
-                    product2(first + j, m, g, sums[first, m][:, g, j, :])
+                    product2(e, m, g, sums[halves[0]][:, g, j, :])
 
-        def store(first, count, m, copy, offset=None):
-            staged = sbuf([P, G, count * U], F32, "staged%d_%d" % (first, m), offset)
+        def layer2_part(part):
+            tag = "codes_turn%d" % (part % 2) if part > 0 else None
+            quantise(hidden_tiles[part], parts[part], "codes%d" % part, tag)
+            layer2(parts[part])
+
+        def store(halves, copy):
+            first, m = halves[0]
+            staged = sbuf([P, G, len(halves) * U], F32, "staged%d_%d" % (first, m))
             copy(staged[:], sums[first, m][:].rearrange("p g j u -> p g (j u)"))
-            columns = slice(first * U, (first + count) * U)
+            columns = slice(first * U, (first + len(halves)) * U)
             nc.sync.dma_start(out_blocks[:, :, m, columns].rearrange("g p c -> p g c"), staged[:])
-
-        def pair_halves(first):
-            return [(first + j, m) for m in range(RANKS) for j in range(2)]
 
         on_vector, on_scalar = nc.vector.tensor_copy, nc.scalar.copy
 
@@ -212,76 +211,61 @@ def tile_moe_pke_mlp_silu_kernel(
         spread_rows(rows_first, x_plane_first)
         nc.sync.dma_start(x_all[:, X_FIRST:T], x_hbm[:, X_FIRST:T])
         load_w1(0, 1)
-        load_w1(1, 3, AT_RAW1)
+        load_w1(1, 3)
         for r in range(ROWS):
             nc.sync.dma_start(s1_plane[r:P:QUAD, :, :], s1_turned[r:P:ROWS, :])
         load_w1(4, 2)
-        x_plane_rest = sbuf([P, (E * C - PAIR) // 4], I32, "x_plane_rest", AT_X_ROWS + E * N)
+        x_plane_rest = sbuf([P, (E * C - PAIR) // 4], I32, "x_plane_rest", offset=E * N)
         spread_rows(rows_rest, x_plane_rest)
         load_w1(6, 2)
-        load_w2(0, 4)
+        load_w2(0, E // 2)
         for r in range(ROWS):
             nc.sync.dma_start(s2_plane[r:P:QUAD, :, :], s2_hbm[r : K // 32 : ROWS, :, :])
-        load_w2(4, 4)
-
-        parts = [[(2 * pair, m), (2 * pair + 1, m)] for pair in range(E // 2) for m in range(RANKS)]
-        tiles = {}
-
-        def layer1_part(part):
-            tiles[part] = new_hidden("hidden%d" % part, parts[part], None)
-            for half in parts[part]:
-                layer1(*half)
-
-        def quantise_part(part):
-            quantise(tiles[part], parts[part], "codes%d" % part, tag="codes_ring%d" % (part % 2) if part else None)
-            layer2(parts[part][0][0], 2, part % RANKS)
-
-        def store_part(part, copy):
-            store(parts[part][0][0], 2, part % RANKS, copy)
+        load_w2(E // 2, E // 2)
 
         gather(0, 1)
-        permute(0, 1, PACK - 1, AT_S1_RAW)
-        permute(1, 1, PACK)
+        permute(0, 1, on_scalar, "s1_raw")
+        permute(1, 1, on_scalar)
         gather(1, 1)
-        gather(2, 2)
-        gather(4, 2)
-        gather(6, 2)
-        permute(2, 2)
-        permute(4, 2)
-        tiles[0] = new_hidden("hidden0", parts[0])
-        tiles[1] = new_hidden("hidden1", parts[1])
+        for first in range(2, E, 2):
+            gather(first, 2)
+        permute_on_gpsimd(2, 2)
+        permute_on_gpsimd(4, 2)
+        for part in range(RANKS):
+            hidden_tiles[part] = new_hidden("hidden%d" % part, parts[part])
         for e in range(2):
             for m in range(RANKS):
                 layer1(e, m)
         for part in range(2, 6):
             layer1_part(part)
-        quantise_part(0)
-        quantise_part(1)
-        permute(6, 2, vector=True)
-        quantise_part(2)
-        store_part(0, on_vector)
-        quantise_part(3)
-        store_part(1, on_vector)
-        store_part(2, on_vector)
+        layer2_part(0)
+        layer2_part(1)
+        permute(6, 2, on_vector)
+        layer2_part(2)
+        store(parts[0], on_vector)
+        layer2_part(3)
+        store(parts[1], on_vector)
+        store(parts[2], on_vector)
+        before_last, last = parts[PARTS - 1]
         layer1_part(6)
-        hidden14 = new_hidden("hidden14", [(6, 1)])
-        layer1(6, 1)
-        quantise_part(4)
-        store_part(3, on_vector)
-        hidden15 = new_hidden("hidden15", [(7, 1)])
-        layer1(7, 1)
-        quantise_part(5)
-        store_part(4, on_vector)
-        quantise_part(6)
-        quantise(hidden14, [(6, 1)], "codes14")
-        layer2(6, 1, 1)
-        quantise(hidden15, [(7, 1)], "codes15")
-        store_part(5, on_scalar)
-        store_part(6, on_vector)
-        store(6, 1, 1, on_scalar)
+        hidden_before_last = new_hidden("hidden_before_last", [before_last])
+        layer1(*before_last)
+        layer2_part(4)
+        store(parts[3], on_vector)
+        hidden_last = new_hidden("hidden_last", [last])
+        layer1(*last)
+        layer2_part(5)
+        store(parts[4], on_vector)
+        layer2_part(6)
+        quantise(hidden_before_last, [before_last], "codes_before_last")
+        layer2([before_last])
+        quantise(hidden_last, [last], "codes_last")
+        store(parts[5], on_scalar)
+        store(parts[6], on_vector)
+        store([before_last], on_scalar)
         for g, (copy, queue) in enumerate(((on_vector, nc.sync), (on_scalar, nc.scalar))):
-            y = bank(RING + g, [P, U], "y")
+            y = bank(SIDE + g, [P, U], "y")
             staged = sbuf([P, U], F32, "staged_last%d" % g)
-            product2(E - 1, 1, g, y[:])
+            product2(E - 1, RANKS - 1, g, y[:])
             copy(staged[:], y[:])
-            queue.dma_start(out_blocks[g, :, 1, (E - 1) * U : E * U], staged[:])
+            queue.dma_start(out_blocks[g, :, RANKS - 1, (E - 1) * U : E * U], staged[:])

@@ -191,8 +191,8 @@ def tile_moe_pke_mlp_silu_kernel(
 
         nc.vector.memset(warm_in[:], 0.0)
         nc.vector.memset(x_rows[0:ROW0, :], 0)
-        nc.gpsimd.memset(x_plane_first[:], 0)
-        nc.gpsimd.memset(s1_plane[:], 0)
+        nc.vector.memset(x_plane_first[:], 0)
+        nc.vector.memset(s1_plane[:], 0)
         nc.sync.dma_start(x_rows[ROW0:P, :], x_scales[0].bitcast(I32))
         nc.sync.dma_start(offsets[:], offs)
         for q, queue in enumerate((nc.sync, nc.sync, nc.scalar, nc.scalar)):

from contextlib import ExitStack

import concourse.mybir as mybir

F32 = mybir.dt.float32
BF16 = mybir.dt.bfloat16
I32 = mybir.dt.int32
U32 = mybir.dt.uint32
U16 = mybir.dt.uint16
U8 = mybir.dt.uint8
FP8X4 = mybir.dt.float8_e4m3fn_x4
FP4X4 = mybir.dt.float4_e2m1fn_x4
SILU = mybir.ActivationFunctionType.Silu

P = 128
PACK = 4
QUAD = 32
ROWS = 4
K, T, E, C, H, N = 512, 4096, 8, 256, 512, 256
RANKS = 2
U = C // RANKS
G = N // P
PAIR = 2 * C
PARTS = E // 2 * RANKS
ROW0 = P - K // 32
X_FIRST = 7 * T // 8
LINE = 8
BANKS = 8
SIDE = BANKS // 2
FLOPS = 2 * E * C * (K * H + H * N)


def tile_moe_pke_mlp_silu_kernel(
    tc, x_words, x_scales, w1_words, w1_scales, w2_words, w2_scales, offs, out
):
    nc = tc.nc
    with ExitStack() as ctx:
        keep = ctx.enter_context(tc.tile_pool(name="keep", bufs=1))
        turns = ctx.enter_context(tc.tile_pool(name="turns", bufs=1))
        psum = ctx.enter_context(tc.psum_pool(name="psum", bufs=1))

        def bank(number, shape, name):
            return psum.tile(shape, F32, name=name, tag="bank%d" % number)

        def sbuf(shape, dtype, name, tag=None, offset=None):
            if offset is not None:
                return turns.tile(shape, dtype, name=name, offset=offset, align_bytes=64)
            return keep.tile(shape, dtype, name=name, tag=tag or name, align_bytes=64)

        offsets = keep.tile([P, E * C // 16], U16, name="offsets")
        x_all = sbuf([P, T], I32, "x_all")
        x_rows = sbuf([P, T // 4], I32, "x_rows", offset=0)
        s1_raw = sbuf([P, H // 4], I32, "s1_raw")
        s1_turned = sbuf([P, H // 4], I32, "s1_turned")
        s1_plane = sbuf([P, E, H // 4], I32, "s1_plane")
        x_plane_first = sbuf([P, PAIR // 4], I32, "x_plane_first")
        warm_in = keep.tile([P, 1], F32, name="warm_in")
        warm_out = keep.tile([P, 1], F32, name="warm_out")
        s2_plane = sbuf([P, E, N // 4], I32, "s2_plane", offset=0)

        x_hbm = x_words[0].rearrange("p t r -> p (t r)").bitcast(I32)
        w1_hbm = w1_words.rearrange("e s p b -> p (e s) b").bitcast(I32)
        w2_hbm = w2_words.rearrange("e s p b -> p (e s) b").bitcast(I32)
        s2_hbm = w2_scales.rearrange("e s q i -> q (e s) i").bitcast(I32)
        out_blocks = out.rearrange("(g p) (m c) -> g p m c", p=P, m=RANKS)
        w1_loads, w1_turned, w2, slot_words, hidden, hidden_tiles, codes, sums = {}, {}, {}, {}, {}, {}, {}, {}
        parts = [[(2 * pair, m), (2 * pair + 1, m)] for pair in range(E // 2) for m in range(RANKS)]
        a_banks = [n % BANKS if n < BANKS + SIDE else SIDE + n % SIDE for n in range(E * RANKS)]
        y_banks = [(SIDE + n) % BANKS for n in range(PARTS)]

        def load_w1(first, count):
            raw = sbuf([P, count, H // 2], I32, "w1_raw%d" % first)
            nc.sync.dma_start(raw[:], w1_hbm[:, first : first + count, :])
            for j in range(count):
                w1_loads[first + j] = (raw, j)

        def load_w2(first, count):
            words = sbuf([P, count, N // 2], I32, "w2_%d" % first)
            nc.sync.dma_start(words[:], w2_hbm[:, first : first + count, :])
            for j in range(count):
                w2[first + j] = words[:, j, :]

        def permute_views(first, count, tag):
            raw, at = w1_loads[first]
            turned = sbuf([P, PACK, count, P // 2], I32, "w1_turned%d" % first, tag)
            for j in range(count):
                w1_turned[first + j] = turned[:, :, j, :]
            return turned[:].bitcast(U16), raw[:, at : at + count, :].bitcast(U16)

        def permute(first, count, copy, tag=None):
            turned, raw = permute_views(first, count, tag)
            copy(
                turned.rearrange("p t e (a b) -> p (e a) t b", b=LINE),
                raw.rearrange("p e (a b t) -> p (e a) t b", b=LINE, t=PACK),
            )

        def permute_on_gpsimd(first, count):
            turned, raw = permute_views(first, count, None)
            nc.gpsimd.tensor_copy(turned, raw.rearrange("p e (m t) -> p t e m", t=PACK))

        def list_piece(first, count):
            return offsets[:, first // 16 : (first + count) // 16]

        def gather_rows(first, count, name):
            rows = sbuf([P, count], U8, name)
            nc.vector.tensor_copy(rows[:], x_rows[:].bitcast(U8).indirect(list_piece(first, count)))
            return rows

        def spread_rows(rows, plane):
            for r in range(ROWS):
                nc.sync.dma_start(plane[r:P:QUAD, :], rows[ROW0 + r : P : ROWS, :].bitcast(I32))

        def gather(first, count):
            words = sbuf([P, count * C], U32, "words%d" % first)
            nc.vector.tensor_copy(words[:], x_all[:].bitcast(U32).indirect(list_piece(first * C, count * C)))
            for j in range(count):
                slot_words[first + j] = words[:, j * C : (j + 1) * C]

        def new_hidden(name, halves):
            tile = sbuf([P, len(halves), U, PACK], BF16, name)
            for n, half in enumerate(halves):
                hidden[half] = tile[:, n, :, :]
            return tile

        def layer1(e, m):
            w1_plane = s1_turned[:] if e == 0 else s1_plane[:, e, :]
            slot = e * C + m * U
            if slot < PAIR:
                x_scale = x_plane_first[:, slot // 4 : (slot + U) // 4]
            else:
                x_scale = x_plane_rest[:, (slot - PAIR) // 4 : (slot - PAIR + U) // 4]
            a = bank(a_banks.pop(0), [P, PACK, U], "a")
            for t in range(PACK):
                nc.tensor.matmul_mx(
                    out=a[:, t, :],
                    lhsT=w1_turned[e][:, t, :].bitcast(FP4X4),
                    lhsT_scale=w1_plane[:, t * P // 4 : (t + 1) * P // 4].bitcast(U8),
                    rhs=slot_words[e][:, m * U : (m + 1) * U].bitcast(FP8X4),
                    rhs_scale=x_scale.bitcast(U8),
                    start=True,
                    stop=True,
                )
            nc.scalar.activation(hidden[e, m], a[:].rearrange("p t u -> p u t"), SILU)

        def layer1_part(part):
            hidden_tiles[part] = new_hidden("hidden%d" % part, parts[part])
            for half in parts[part]:
                layer1(*half)

        def quantise(tile, halves, name, tag=None):
            width = len(halves) * U
            h_words = sbuf([P, width], U32, name, tag)
            h_plane = sbuf([P, width], U8, name + "_plane")
            nc.vector.quantize_mx(
                out=h_words[:].bitcast(FP8X4), scales=h_plane[:], in_=tile[:].rearrange("p n u t -> p (n u t)")
            )
            for n, half in enumerate(halves):
                codes[half] = (h_words[:, n * U : (n + 1) * U], h_plane[:, n * U : (n + 1) * U])

        def product2(e, m, g, y):
            h_words, h_plane = codes[e, m]
            nc.tensor.matmul_mx(
                out=y,
                lhsT=w2[e][:, g * P // 2 : (g + 1) * P // 2].bitcast(FP4X4),
                lhsT_scale=s2_plane[:, e, g * P // 4 : (g + 1) * P // 4].bitcast(U8),
                rhs=h_words.bitcast(FP8X4),
                rhs_scale=h_plane,
                start=True,
                stop=True,
            )

        def layer2(halves):
            sums[halves[0]] = bank(y_banks.pop(0), [P, G, len(halves), U], "y")
            for j, (e, m) in enumerate(halves):
                for g in range(G):
                    product2(e, m, g, sums[halves[0]][:, g, j, :])

        def layer2_part(part):
            tag = "codes_turn%d" % (part % 2) if part > 0 else None
            quantise(hidden_tiles[part], parts[part], "codes%d" % part, tag)
            layer2(parts[part])

        def store(halves, copy):
            first, m = halves[0]
            staged = sbuf([P, G, len(halves) * U], F32, "staged%d_%d" % (first, m))
            copy(staged[:], sums[first, m][:].rearrange("p g j u -> p g (j u)"))
            columns = slice(first * U, (first + len(halves)) * U)
            nc.sync.dma_start(out_blocks[:, :, m, columns].rearrange("g p c -> p g c"), staged[:])

        on_vector, on_scalar = nc.vector.tensor_copy, nc.scalar.copy

        nc.vector.memset(warm_in[:], 0.0)
        nc.vector.memset(x_rows[0:ROW0, :], 0)
        nc.vector.memset(x_plane_first[:], 0)
        nc.vector.memset(s1_plane[:], 0)
        nc.sync.dma_start(x_rows[ROW0:P, :], x_scales[0].bitcast(I32))
        nc.sync.dma_start(offsets[:], offs)
        for q, queue in enumerate((nc.sync, nc.sync, nc.scalar, nc.scalar)):
            queue.dma_start(
                s1_raw[QUAD * q : QUAD * (q + 1), :], w1_scales[:, 0, ROWS * q : ROWS * (q + 1), :].bitcast(I32)
            )
        nc.sync.dma_start(x_all[:, 0:X_FIRST], x_hbm[:, 0:X_FIRST])
        nc.scalar.activation(warm_out[:], warm_in[:], SILU)

        nc.gpsimd.tensor_copy(
            s1_turned[:].bitcast(U8).rearrange("p (t m) -> p t m", t=PACK),
            s1_raw[:].bitcast(U8).rearrange("p (m t) -> p t m", t=PACK),
        )
        rows_first = gather_rows(0, PAIR, "rows_first")
        rows_rest = gather_rows(PAIR, E * C - PAIR, "rows_rest")
        spread_rows(rows_first, x_plane_first)
        nc.sync.dma_start(x_all[:, X_FIRST:T], x_hbm[:, X_FIRST:T])
        load_w1(0, 1)
        load_w1(1, 3)
        for r in range(ROWS):
            nc.sync.dma_start(s1_plane[r:P:QUAD, :, :], s1_turned[r:P:ROWS, :])
        load_w1(4, 2)
        x_plane_rest = sbuf([P, (E * C - PAIR) // 4], I32, "x_plane_rest", offset=E * N)
        spread_rows(rows_rest, x_plane_rest)
        load_w1(6, 2)
        load_w2(0, E // 2)
        for r in range(ROWS):
            nc.sync.dma_start(s2_plane[r:P:QUAD, :, :], s2_hbm[r : K // 32 : ROWS, :, :])
        load_w2(E // 2, E // 2)

        gather(0, 1)
        permute(0, 1, on_scalar, "s1_raw")
        permute(1, 1, on_scalar)
        gather(1, 1)
        for first in range(2, E, 2):
            gather(first, 2)
        permute_on_gpsimd(2, 2)
        permute_on_gpsimd(4, 2)
        for part in range(RANKS):
            hidden_tiles[part] = new_hidden("hidden%d" % part, parts[part])
        for e in range(2):
            for m in range(RANKS):
                layer1(e, m)
        for part in range(2, 6):
            layer1_part(part)
        layer2_part(0)
        layer2_part(1)
        permute(6, 2, on_vector)
        layer2_part(2)
        store(parts[0], on_vector)
        layer2_part(3)
        store(parts[1], on_vector)
        store(parts[2], on_vector)
        before_last, last = parts[PARTS - 1]
        layer1_part(6)
        hidden_before_last = new_hidden("hidden_before_last", [before_last])
        layer1(*before_last)
        layer2_part(4)
        store(parts[3], on_vector)
        hidden_last = new_hidden("hidden_last", [last])
        layer1(*last)
        layer2_part(5)
        store(parts[4], on_vector)
        layer2_part(6)
        quantise(hidden_before_last, [before_last], "codes_before_last")
        layer2([before_last])
        quantise(hidden_last, [last], "codes_last")
        store(parts[5], on_scalar)
        store(parts[6], on_vector)
        store([before_last], on_scalar)
        for g, (copy, queue) in enumerate(((on_vector, nc.sync), (on_scalar, nc.scalar))):
            y = bank(SIDE + g, [P, U], "y")
            staged = sbuf([P, U], F32, "staged_last%d" % g)
            product2(E - 1, RANKS - 1, g, y[:])
            copy(staged[:], y[:])
            queue.dma_start(out_blocks[g, :, RANKS - 1, (E - 1) * U : E * U], staged[:])
